import numpy as np
import ml_dtypes


def mxq(x, axis, fmt="e4m3"):
    dtype, down = {"e4m3": (ml_dtypes.float8_e4m3fn, 7), "e5m2": (ml_dtypes.float8_e5m2, 14)}[fmt]
    v = np.moveaxis(np.asarray(x, np.float32).astype(ml_dtypes.bfloat16).astype(np.float64), axis, -1)
    blocks = v.reshape(v.shape[:-1] + (-1, 32))
    amax = np.abs(blocks).max(-1, keepdims=True)
    byte = np.maximum(np.where(amax > 0, np.frexp(amax)[1] - 1 + 127, 0) - down, 1)
    scale = np.exp2(byte - 127.0)
    codes = (blocks / scale).astype(np.float32).astype(dtype).astype(np.float64)
    return np.moveaxis((codes * scale).reshape(v.shape), -1, axis)


WIDE = False


def mx_kscale(k):
    if not WIDE:
        return np.ones(k)
    levels = np.array([24, -24, 12, -12, 0])
    if k % 512:
        return np.exp2(np.random.permutation(np.resize(levels, k // 32))).repeat(32)
    a = np.empty((k // 512, 16))
    for p in range(k // 512):
        a[p, :8] = np.random.permutation(np.resize(levels, 8))
        for g in range(8):
            far = levels[np.abs(levels - a[p, g]) >= 10]
            a[p, g + 8] = far[np.random.randint(len(far))]
    return np.exp2(a.ravel()).repeat(32)


def f64(x):
    return np.asarray(x).astype(np.float64)


def striped8(idx):
    return np.concatenate([v.reshape(-1, 16).T for v in idx]).astype(np.uint16)


def unstriped8(offs):
    return np.stack([offs[16 * g:16 * g + 16].T.reshape(-1) for g in range(8)]).astype(np.int64)


E2M1 = np.array([0.0, 0.5, 1.0, 1.5, 2.0, 3.0, 4.0, 6.0, -0.0, -0.5, -1.0, -1.5, -2.0, -3.0, -4.0, -6.0])


def pack_weight(w, fmt):
    k, n = w.shape
    w = f64(np.asarray(w, np.float32).astype(ml_dtypes.bfloat16)).reshape(k // 32, 32, n)
    amax = np.abs(w).max(1)
    if fmt == "e4m3":
        byte = np.frexp(amax)[1] - 1 + 127 - 7
    else:
        mant, ex = np.frexp(amax / 6.0)
        byte = np.where(mant > 0.5, ex, ex - 1) + 127
    byte = np.clip(np.where(amax > 0, byte, 1), 1, 254)
    scaled = (w * np.exp2(127.0 - byte)[:, None, :]).reshape(k, n).astype(np.float32)
    by_word = np.ascontiguousarray(scaled.reshape(k // 512, 128, 4, n).transpose(0, 1, 3, 2))
    if fmt == "e4m3":
        words = by_word.astype(ml_dtypes.float8_e4m3fn).view(np.uint8)
    else:
        c = by_word.astype(ml_dtypes.float4_e2m1fn).view(np.uint8) & 0xF
        words = (c[..., 0::2] | (c[..., 1::2] << 4)).reshape(k // 512, 128, 2 * n)
    return np.ascontiguousarray(words), np.ascontiguousarray(byte.astype(np.uint8).reshape(k // 512, 16, n))


def unpack_weight(words, scales, fmt):
    g, _, n = scales.shape
    words = np.ascontiguousarray(words).reshape(g, 128, n, -1)
    if fmt == "e4m3":
        vals = words.view(ml_dtypes.float8_e4m3fn).astype(np.float64)
    else:
        nib = np.empty((g, 128, n, 4), np.uint8)
        nib[..., 0::2] = words & 0xF
        nib[..., 1::2] = words >> 4
        vals = E2M1[nib]
    vals = vals * np.repeat(np.exp2(scales.astype(np.float64) - 127.0), 8, axis=1)[..., None]
    return vals.transpose(0, 1, 3, 2).reshape(g * 512, n)


def planes(y):
    n, m = y.shape
    v = y.astype(np.float32).astype(ml_dtypes.bfloat16).astype(np.float64).reshape(n // 32, 32, m)
    top = np.abs(v).max(1)
    byte = np.clip(np.where(top > 0, np.frexp(top)[1] - 1 + 127 - 7, 1), 1, 254)
    codes = (v * np.exp2(127.0 - byte)[:, None, :]).reshape(n, m).astype(np.float32).astype(ml_dtypes.float8_e4m3fn).view(np.uint8)
    words = codes.reshape(n // 512, 128, 4, m).transpose(0, 1, 3, 2)
    return np.ascontiguousarray(words), np.ascontiguousarray(byte.astype(np.uint8).reshape(n // 512, 16, m))


def gelu(f):
    return 0.5 * f * (1.0 + np.tanh(np.sqrt(2.0 / np.pi) * (f + 0.044715 * f**3)))


K, N, T, J = 512, 512, 2048, 512


def setup_inputs():
    n = np.random.standard_normal
    s = mx_kscale(K)[:, None]
    p_w4 = pack_weight(n((K, N)) / np.sqrt(K) / s, "e2m1")
    return {
        "xT": (n((K, T)) * s).astype(np.float32),
        "wgt": np.repeat(np.random.uniform(0.5, 2.0, (8, 3 * J)), 16, axis=0).astype(np.float32),
        "w4_words": p_w4[0],
        "w4_scales": p_w4[1],
        "wd": (0.4 * (n((K, N)) / np.sqrt(K) / s)).astype(np.float32),
        "iw0": (np.random.uniform(0.1, 0.9, (N, J))).astype(np.float32),
        "iw1": (np.random.uniform(0.1, 0.9, (N, J))).astype(np.float32),
        "iw2": (np.random.uniform(0.1, 0.9, (N, J))).astype(np.float32),
        "b": (0.3 * n(N)).astype(np.float32),
        "offs": striped8(np.stack([np.concatenate([np.random.permutation(T)[:J] for _ in range(3)]) for _ in range(8)])),
    }


def reference(xT, wgt, w4_words, w4_scales, wd, iw0, iw1, iw2, b, offs):
    idx = unstriped8(offs)
    rows = np.arange(K)
    xg = f64(wgt)[rows // 4 % 128] * f64(xT)[rows[:, None], idx[rows % 512 // 64]]
    xT_ = mxq(xg, 0, "e4m3").reshape(K, 3, J)
    w4_ = unpack_weight(w4_words, w4_scales, "e2m1")
    wd_ = mxq(f64(wd), 0, "e4m3")
    a0 = w4_.T @ xT_[:, 0] + wd_.T @ xT_[:, 0]
    a1 = w4_.T @ xT_[:, 1] + wd_.T @ xT_[:, 1]
    a2 = w4_.T @ xT_[:, 2] + wd_.T @ xT_[:, 2]
    out_0 = gelu(a0 * f64(iw0) + a1 * f64(iw1) + a2 * f64(iw2) + f64(b)[:, None])
    return (out_0,) + planes(out_0)

@@ -1,0 +1,226 @@
+from contextlib import ExitStack
+
+import concourse.mybir as mybir
+
+K, N, T, J = 512, 512, 2048, 512
+PICKS = 3
+P = 128
+PACK = 4
+JB = 128
+FLOPS = 2 * 2 * K * N * PICKS * J
+
+F32 = mybir.dt.float32
+BF16 = mybir.dt.bfloat16
+I32 = mybir.dt.int32
+U32 = mybir.dt.uint32
+U16 = mybir.dt.uint16
+U8 = mybir.dt.uint8
+FP8X4 = mybir.dt.float8_e4m3fn_x4
+FP4X4 = mybir.dt.float4_e2m1fn_x4
+MULT = mybir.AluOpType.mult
+ADD = mybir.AluOpType.add
+GELU = mybir.ActivationFunctionType.Gelu_apprx_tanh
+
+
+def tile_list_dl_soft_geluP_kernel(
+    tc, xT, wgt, w4_words, w4_scales, wd, iw0, iw1, iw2, b, offs, out_0, out_1, out_2
+):
+    nc = tc.nc
+    with ExitStack() as ctx:
+        keep = ctx.enter_context(tc.tile_pool(name="keep", bufs=1))
+        psum = ctx.enter_context(tc.psum_pool(name="psum", bufs=1))
+
+        def sb(name, shape, dtype):
+            return keep.tile(shape, dtype, name=name, align_bytes=64)
+
+        offsets = keep.tile([P, PICKS * J // 16], U16, name="offsets")
+        x_rows = xT.rearrange("(p i) t -> i p t", i=PACK)
+        x_sb = [sb("x%d" % i, [P, T], F32) for i in range(PACK)]
+        wgt_sb = [sb("wgt%d" % c, [P, J], F32) for c in range(PICKS)]
+        wd_sb = sb("wd", [P, PACK, N], F32)
+        iw_sb = [sb("iw%d" % c, [P, PACK, J], F32) for c in range(PICKS)]
+        w4_raw = sb("w4_raw", [P, 2 * N], U8)
+        s4_raw = sb("s4_raw", [P, N], U8)
+        bias = sb("bias", [P, PACK], F32)
+
+        def load_wgt(c):
+            nc.sync.dma_start(wgt_sb[c][:], wgt[:, c * J : (c + 1) * J])
+
+        def load_x(i):
+            nc.sync.dma_start(x_sb[i][:], x_rows[i])
+
+        nc.vector.memset(s4_raw[:].bitcast(I32), 0)
+        nc.sync.dma_start(offsets[:], offs)
+        load_wgt(0)
+        load_x(0)
+        nc.scalar.dma_start(w4_raw[:].bitcast(I32), w4_words[0].bitcast(I32))
+        for q in range(4):
+            nc.scalar.dma_start(
+                s4_raw[32 * q : 32 * q + 4, :].bitcast(I32), w4_scales[0, 4 * q : 4 * q + 4, :].bitcast(I32)
+            )
+        nc.scalar.dma_start(bias[:], b.rearrange("(p t) -> p t", t=PACK))
+        load_wgt(1)
+        load_x(1)
+        load_x(2)
+        load_x(3)
+        load_wgt(2)
+        nc.sync.dma_start(wd_sb[:], wd.rearrange("(p i) n -> p i n", i=PACK))
+        for c, iw in enumerate((iw0, iw1, iw2)):
+            nc.sync.dma_start(iw_sb[c][:], iw.rearrange("(p t) j -> p t j", t=PACK))
+
+        w4_codes = sb("w4_codes", [P, 2 * N], U8)
+        w4_sc = sb("w4_sc", [P, N], U8)
+        nc.vector.tensor_copy(
+            w4_codes[:].rearrange("p (t m e) -> p t m e", t=PACK, e=2),
+            w4_raw[:].rearrange("p (m t e) -> p t m e", t=PACK, e=2),
+        )
+        nc.vector.tensor_copy(
+            w4_sc[:].rearrange("p (t m) -> p t m", t=PACK),
+            s4_raw[:].rearrange("p (m t) -> p t m", t=PACK),
+        )
+
+        late = sb("late", [P, PACK * 2 * J], F32)
+        picked = [sb("picked%d" % c, [P, PACK, J], F32)[:] for c in range(PICKS - 1)]
+        picked.append(late[:].rearrange("p (i w) -> p i w", i=PACK)[:, :, 0:J])
+        xg_bf = [late[:, 4 * J : 6 * J].bitcast(BF16)]
+        xg_bf.extend(sb("xg_bf%d" % c, [P, J * PACK], BF16)[:] for c in range(1, PICKS))
+        xg_codes = [sb("xg_codes%d" % c, [P, J], U32) for c in range(PICKS)]
+        xg_sc = [sb("xg_sc%d" % c, [P, J], U8) for c in range(PICKS)]
+        wd_bf = late[:, 6 * J : 8 * J].bitcast(BF16)
+        wd_codes = sb("wd_codes", [P, N], U32)
+        wd_sc = sb("wd_sc", [P, N], U8)
+
+        def gather(c, i):
+            cols = J // 16
+            nc.vector.tensor_tensor(
+                picked[c][:, i, :],
+                x_sb[i][:].indirect(offsets[:, c * cols : (c + 1) * cols]),
+                wgt_sb[c][:],
+                MULT,
+            )
+
+        def weave_x(c):
+            nc.scalar.copy(
+                xg_bf[c].rearrange("p (g r i) -> p g i r", r=4, i=PACK),
+                picked[c].rearrange("p i (g r) -> p g i r", r=4),
+            )
+
+        def quantize_x(c):
+            nc.vector.quantize_mx(out=xg_codes[c][:].bitcast(FP8X4), scales=xg_sc[c][:], in_=xg_bf[c])
+
+        def base_pass(out, c, t, j0, width):
+            nc.tensor.matmul_mx(
+                out=out,
+                lhsT=w4_codes[:, 2 * P * t : 2 * P * (t + 1)].bitcast(FP4X4),
+                lhsT_scale=w4_sc[:, P * t : P * (t + 1)],
+                rhs=xg_codes[c][:, j0 : j0 + width].bitcast(FP8X4),
+                rhs_scale=xg_sc[c][:, j0 : j0 + width],
+                start=True,
+                stop=False,
+            )
+
+        def delta_pass(out, c, t, j0, width):
+            nc.tensor.matmul_mx(
+                out=out,
+                lhsT=wd_codes[:, P * t : P * (t + 1)].bitcast(FP8X4),
+                lhsT_scale=wd_sc[:, P * t : P * (t + 1)],
+                rhs=xg_codes[c][:, j0 : j0 + width].bitcast(FP8X4),
+                rhs_scale=xg_sc[c][:, j0 : j0 + width],
+                start=False,
+                stop=True,
+            )
+
+        def project(out, c, t, j0, width):
+            base_pass(out, c, t, j0, width)
+            delta_pass(out, c, t, j0, width)
+
+        for i in range(PACK):
+            gather(0, i)
+            gather(1, i)
+        weave_x(0)
+        nc.scalar.copy(
+            wd_bf.rearrange("p (t m i) -> p m i t", t=PACK, i=PACK),
+            wd_sb[:].rearrange("p i (m t) -> p m i t", t=PACK),
+        )
+        weave_x(1)
+        gather(2, 0)
+        gather(2, 1)
+        quantize_x(0)
+        gather(2, 2)
+        nc.vector.quantize_mx(out=wd_codes[:].bitcast(FP8X4), scales=wd_sc[:], in_=wd_bf)
+        gather(2, 3)
+        weave_x(2)
+
+        def bank(index):
+            return psum.tile([P, 512], F32, name="bank%d" % index)
+
+        pooled0 = [sb("pooled0_%d" % t, [P, J], F32) for t in range(PACK)]
+        pooled1 = [sb("pooled1_%d" % t, [P, J], F32) for t in range(PACK)]
+        partial = sb("partial", [P, PACK, J], F32)
+        acc0 = [bank(t) for t in range(PACK)]
+        for t in range(PACK):
+            base_pass(acc0[t][:], 0, t, 0, J)
+        for t in range(PACK):
+            delta_pass(acc0[t][:], 0, t, 0, J)
+        quantize_x(1)
+        acc1 = [bank(PACK + t) for t in range(PACK)]
+        for t in range(PACK):
+            project(acc1[t][:], 1, t, 0, J)
+        for t in range(PACK):
+            nc.vector.tensor_tensor(pooled0[t][:], acc0[t][:], iw_sb[0][:, t, :], MULT)
+        quantize_x(2)
+        for t in range(PACK):
+            nc.vector.tensor_tensor(pooled1[t][:], acc1[t][:], iw_sb[1][:, t, :], MULT)
+        for t in range(PACK):
+            nc.vector.scalar_tensor_tensor(
+                partial[:, t, :], pooled0[t][:], bias[:, t : t + 1], pooled1[t][:], ADD, ADD
+            )
+
+        y_sc = sb("y_sc", [P, J], U8)
+        y_rows = out_0.rearrange("(p t) j -> p t j", t=PACK)
+        y_words = out_1[0].rearrange("p j i -> p (j i)").bitcast(I32)
+        blocks = J // JB
+        acc2 = [bank(u) for u in range(blocks)]
+        pooled2 = [sb("pooled2_%d" % u, [P, PACK, JB], F32) for u in range(blocks)]
+        total = [sb("total%d" % u, [P, PACK, JB], F32) for u in range(blocks)]
+        y_f32 = [sb("y_f32_%d" % u, [P, PACK, JB], F32) for u in range(blocks)]
+        y_bf = [sb("y_bf%d" % u, [P, JB * PACK], BF16) for u in range(blocks)]
+        y_codes = [sb("y_codes%d" % u, [P, JB], U32) for u in range(blocks)]
+
+        def pool_last(u):
+            js = slice(u * JB, (u + 1) * JB)
+            nc.vector.tensor_tensor(
+                pooled2[u][:], acc2[u][:].rearrange("p (t j) -> p t j", t=PACK), iw_sb[2][:, :, js], MULT
+            )
+
+        def finish(u):
+            js = slice(u * JB, (u + 1) * JB)
+            nc.vector.tensor_tensor(total[u][:], pooled2[u][:], partial[:, :, js], ADD)
+            nc.scalar.activation(
+                y_bf[u][:].rearrange("p (g r t) -> p g t r", r=4, t=PACK),
+                total[u][:].rearrange("p t (g r) -> p g t r", r=4),
+                GELU,
+            )
+            nc.scalar.activation(y_f32[u][:], total[u][:], GELU)
+            nc.scalar.dma_start(y_rows[:, :, js], y_f32[u][:])
+
+        def hand_on(u):
+            js = slice(u * JB, (u + 1) * JB)
+            nc.vector.quantize_mx(out=y_codes[u][:].bitcast(FP8X4), scales=y_sc[:, js], in_=y_bf[u][:])
+            nc.sync.dma_start(y_words[:, js], y_codes[u][:].bitcast(I32))
+
+        for u in range(blocks):
+            for t in range(PACK):
+                project(acc2[u][:, t * JB : (t + 1) * JB], 2, t, u * JB, JB)
+        pool_last(0)
+        for u in range(blocks):
+            if u + 1 < blocks:
+                pool_last(u + 1)
+            finish(u)
+            if u >= 1:
+                hand_on(u - 1)
+        hand_on(blocks - 1)
+        for q in range(4):
+            nc.sync.dma_start(
+                out_2[0, 4 * q : 4 * q + 4, :].bitcast(I32), y_sc[32 * q : 32 * q + 4, :].bitcast(I32)
+            )

@@ -30,8 +30,8 @@ def tile_list_dl_soft_geluP_kernel(
         keep = ctx.enter_context(tc.tile_pool(name="keep", bufs=1))
         psum = ctx.enter_context(tc.psum_pool(name="psum", bufs=1))
 
-        def sb(name, shape, dtype):
-            return keep.tile(shape, dtype, name=name, align_bytes=64)
+        def sb(name, shape, dtype, tag=None):
+            return keep.tile(shape, dtype, name=name, tag=tag or name, align_bytes=64)
 
         offsets = keep.tile([P, PICKS * J // 16], U16, name="offsets")
         x_rows = xT.rearrange("(p i) t -> i p t", i=PACK)
@@ -54,19 +54,13 @@ def tile_list_dl_soft_geluP_kernel(
         load_wgt(0)
         load_x(0)
         nc.scalar.dma_start(w4_raw[:].bitcast(I32), w4_words[0].bitcast(I32))
-        for q in range(4):
-            nc.scalar.dma_start(
-                s4_raw[32 * q : 32 * q + 4, :].bitcast(I32), w4_scales[0, 4 * q : 4 * q + 4, :].bitcast(I32)
-            )
-        nc.scalar.dma_start(bias[:], b.rearrange("(p t) -> p t", t=PACK))
+        nc.scalar.dma_start(s4_raw[0:16, :].bitcast(I32), w4_scales[0].bitcast(I32))
         load_wgt(1)
+        load_wgt(2)
         load_x(1)
         load_x(2)
-        load_x(3)
-        load_wgt(2)
         nc.sync.dma_start(wd_sb[:], wd.rearrange("(p i) n -> p i n", i=PACK))
-        for c, iw in enumerate((iw0, iw1, iw2)):
-            nc.sync.dma_start(iw_sb[c][:], iw.rearrange("(p t) j -> p t j", t=PACK))
+        load_x(3)
 
         w4_codes = sb("w4_codes", [P, 2 * N], U8)
         w4_sc = sb("w4_sc", [P, N], U8)
@@ -79,15 +73,22 @@ def tile_list_dl_soft_geluP_kernel(
             s4_raw[:].rearrange("p (m t) -> p t m", t=PACK),
         )
 
-        late = sb("late", [P, PACK * 2 * J], F32)
+        for q in range(1, 4):
+            nc.gpsimd.dma_start(w4_sc[32 * q : 32 * q + 4, :].bitcast(I32), w4_sc[4 * q : 4 * q + 4, :].bitcast(I32))
+        nc.gpsimd.dma_start(bias[:], b.rearrange("(p t) -> p t", t=PACK))
+        for c, iw in enumerate((iw0, iw1, iw2)):
+            nc.sync.dma_start(iw_sb[c][:], iw.rearrange("(p t) j -> p t j", t=PACK))
+
+        pitch = 5 * J // 2
+        late = sb("late", [P, PACK * pitch], F32)
         picked = [sb("picked%d" % c, [P, PACK, J], F32)[:] for c in range(PICKS - 1)]
         picked.append(late[:].rearrange("p (i w) -> p i w", i=PACK)[:, :, 0:J])
-        xg_bf = [late[:, 4 * J : 6 * J].bitcast(BF16)]
+        seam = 3 * pitch + J // 2
+        xg_bf = [late[:, seam - 2 * J : seam].bitcast(BF16)]
         xg_bf.extend(sb("xg_bf%d" % c, [P, J * PACK], BF16)[:] for c in range(1, PICKS))
         xg_codes = [sb("xg_codes%d" % c, [P, J], U32) for c in range(PICKS)]
         xg_sc = [sb("xg_sc%d" % c, [P, J], U8) for c in range(PICKS)]
-        wd_bf = late[:, 6 * J : 8 * J].bitcast(BF16)
-        wd_codes = sb("wd_codes", [P, N], U32)
+        wd_bf = late[:, seam : seam + 2 * J].bitcast(BF16)
         wd_sc = sb("wd_sc", [P, N], U8)
 
         def gather(c, i):
@@ -103,6 +104,12 @@ def tile_list_dl_soft_geluP_kernel(
             nc.scalar.copy(
                 xg_bf[c].rearrange("p (g r i) -> p g i r", r=4, i=PACK),
                 picked[c].rearrange("p i (g r) -> p g i r", r=4),
+            )
+
+        def weave_pair(c, u):
+            nc.scalar.copy(
+                xg_bf[c].rearrange("p (j u e) -> p u j e", u=2, e=2)[:, u],
+                picked[c][:, 2 * u : 2 * u + 2, :].rearrange("p e j -> p j e"),
             )
 
         def quantize_x(c):
@@ -134,20 +141,23 @@ def tile_list_dl_soft_geluP_kernel(
             base_pass(out, c, t, j0, width)
             delta_pass(out, c, t, j0, width)
 
-        for i in range(PACK):
-            gather(0, i)
-            gather(1, i)
-        weave_x(0)
+        for i in range(PACK - 1):
+            for c in range(PICKS):
+                gather(c, i)
+            if i == 1:
+                weave_pair(0, 0)
+                weave_pair(1, 0)
         nc.scalar.copy(
             wd_bf.rearrange("p (t m i) -> p m i t", t=PACK, i=PACK),
             wd_sb[:].rearrange("p i (m t) -> p m i t", t=PACK),
         )
-        weave_x(1)
-        gather(2, 0)
-        gather(2, 1)
-        quantize_x(0)
-        gather(2, 2)
+        gather(0, 3)
+        gather(1, 3)
+        weave_pair(0, 1)
+        weave_pair(1, 1)
+        wd_codes = sb("wd_codes", [P, N], U32, tag="wgt1")
         nc.vector.quantize_mx(out=wd_codes[:].bitcast(FP8X4), scales=wd_sc[:], in_=wd_bf)
+        quantize_x(0)
         gather(2, 3)
         weave_x(2)
 
@@ -159,9 +169,7 @@ def tile_list_dl_soft_geluP_kernel(
         partial = sb("partial", [P, PACK, J], F32)
         acc0 = [bank(t) for t in range(PACK)]
         for t in range(PACK):
-            base_pass(acc0[t][:], 0, t, 0, J)
-        for t in range(PACK):
-            delta_pass(acc0[t][:], 0, t, 0, J)
+            project(acc0[t][:], 0, t, 0, J)
         quantize_x(1)
         acc1 = [bank(PACK + t) for t in range(PACK)]
         for t in range(PACK):
@@ -182,10 +190,11 @@ def tile_list_dl_soft_geluP_kernel(
         blocks = J // JB
         acc2 = [bank(u) for u in range(blocks)]
         pooled2 = [sb("pooled2_%d" % u, [P, PACK, JB], F32) for u in range(blocks)]
-        total = [sb("total%d" % u, [P, PACK, JB], F32) for u in range(blocks)]
-        y_f32 = [sb("y_f32_%d" % u, [P, PACK, JB], F32) for u in range(blocks)]
-        y_bf = [sb("y_bf%d" % u, [P, JB * PACK], BF16) for u in range(blocks)]
-        y_codes = [sb("y_codes%d" % u, [P, JB], U32) for u in range(blocks)]
+        pieces = [(u * JB, JB) for u in range(blocks - 1)] + [(J - JB, JB // 2), (J - JB // 2, JB // 2)]
+        total = [sb("total%d" % v, [P, PACK, w], F32) for v, (j0, w) in enumerate(pieces)]
+        y_f32 = [sb("y_f32_%d" % v, [P, PACK, w], F32) for v, (j0, w) in enumerate(pieces)]
+        y_bf = [sb("y_bf%d" % v, [P, w * PACK], BF16) for v, (j0, w) in enumerate(pieces)]
+        y_codes = sb("y_codes", [P, J], U32)
 
         def pool_last(u):
             js = slice(u * JB, (u + 1) * JB)
@@ -193,34 +202,40 @@ def tile_list_dl_soft_geluP_kernel(
                 pooled2[u][:], acc2[u][:].rearrange("p (t j) -> p t j", t=PACK), iw_sb[2][:, :, js], MULT
             )
 
-        def finish(u):
-            js = slice(u * JB, (u + 1) * JB)
-            nc.vector.tensor_tensor(total[u][:], pooled2[u][:], partial[:, :, js], ADD)
+        def finish(v):
+            j0, w = pieces[v]
+            js = slice(j0, j0 + w)
+            nc.vector.tensor_tensor(
+                total[v][:], pooled2[j0 // JB][:, :, j0 % JB : j0 % JB + w], partial[:, :, js], ADD
+            )
             nc.scalar.activation(
-                y_bf[u][:].rearrange("p (g r t) -> p g t r", r=4, t=PACK),
-                total[u][:].rearrange("p t (g r) -> p g t r", r=4),
+                y_bf[v][:].rearrange("p (g r t) -> p g t r", r=4, t=PACK),
+                total[v][:].rearrange("p t (g r) -> p g t r", r=4),
                 GELU,
             )
-            nc.scalar.activation(y_f32[u][:], total[u][:], GELU)
-            nc.scalar.dma_start(y_rows[:, :, js], y_f32[u][:])
+            nc.scalar.activation(y_f32[v][:], total[v][:], GELU)
+            nc.sync.dma_start(y_rows[:, :, js], y_f32[v][:])
 
-        def hand_on(u):
-            js = slice(u * JB, (u + 1) * JB)
-            nc.vector.quantize_mx(out=y_codes[u][:].bitcast(FP8X4), scales=y_sc[:, js], in_=y_bf[u][:])
-            nc.sync.dma_start(y_words[:, js], y_codes[u][:].bitcast(I32))
+        def hand_on(v):
+            j0, w = pieces[v]
+            js = slice(j0, j0 + w)
+            nc.vector.quantize_mx(out=y_codes[:, js].bitcast(FP8X4), scales=y_sc[:, js], in_=y_bf[v][:])
+            if j0 + w == J - JB:
+                nc.sync.dma_start(y_words[:, 0 : J - JB], y_codes[:, 0 : J - JB].bitcast(I32))
+            if j0 + w == J:
+                nc.sync.dma_start(y_words[:, J - JB : J], y_codes[:, J - JB : J].bitcast(I32))
 
         for u in range(blocks):
             for t in range(PACK):
                 project(acc2[u][:, t * JB : (t + 1) * JB], 2, t, u * JB, JB)
         pool_last(0)
-        for u in range(blocks):
-            if u + 1 < blocks:
-                pool_last(u + 1)
-            finish(u)
-            if u >= 1:
-                hand_on(u - 1)
-        hand_on(blocks - 1)
+        for v in range(len(pieces)):
+            if v + 1 < blocks:
+                pool_last(v + 1)
+            finish(v)
+            if v >= 1:
+                hand_on(v - 1)
+        hand_on(len(pieces) - 1)
         for q in range(4):
-            nc.sync.dma_start(
-                out_2[0, 4 * q : 4 * q + 4, :].bitcast(I32), y_sc[32 * q : 32 * q + 4, :].bitcast(I32)
-            )
+            queue = nc.scalar if q % 2 else nc.sync
+            queue.dma_start(out_2[0, 4 * q : 4 * q + 4, :].bitcast(I32), y_sc[32 * q : 32 * q + 4, :].bitcast(I32))

@@ -19,6 +19,7 @@ FP8X4 = mybir.dt.float8_e4m3fn_x4
 FP4X4 = mybir.dt.float4_e2m1fn_x4
 MULT = mybir.AluOpType.mult
 ADD = mybir.AluOpType.add
+IDENTITY = mybir.ActivationFunctionType.Identity
 GELU = mybir.ActivationFunctionType.Gelu_apprx_tanh
 
 
@@ -38,7 +39,6 @@ def tile_list_dl_soft_geluP_kernel(
         x_sb = [sb("x%d" % i, [P, T], F32) for i in range(PACK)]
         wgt_sb = [sb("wgt%d" % c, [P, J], F32) for c in range(PICKS)]
         wd_sb = sb("wd", [P, PACK, N], F32)
-        iw_sb = [sb("iw%d" % c, [P, PACK, J], F32) for c in range(PICKS)]
         w4_raw = sb("w4_raw", [P, 2 * N], U8)
         s4_raw = sb("s4_raw", [P, N], U8)
         bias = sb("bias", [P, PACK], F32)
@@ -74,10 +74,15 @@ def tile_list_dl_soft_geluP_kernel(
         )
 
         for q in range(1, 4):
-            nc.gpsimd.dma_start(w4_sc[32 * q : 32 * q + 4, :].bitcast(I32), w4_sc[4 * q : 4 * q + 4, :].bitcast(I32))
-        nc.gpsimd.dma_start(bias[:], b.rearrange("(p t) -> p t", t=PACK))
-        for c, iw in enumerate((iw0, iw1, iw2)):
-            nc.sync.dma_start(iw_sb[c][:], iw.rearrange("(p t) j -> p t j", t=PACK))
+            nc.sync.dma_start(w4_sc[32 * q : 32 * q + 4, :].bitcast(I32), w4_sc[4 * q : 4 * q + 4, :].bitcast(I32))
+        nc.sync.dma_start(bias[:], b.rearrange("(p t) -> p t", t=PACK))
+        iw_sb = []
+
+        def load_iw(iw, after):
+            iw_sb.append(sb("iw%d" % len(iw_sb), [P, PACK, J], F32, tag=after))
+            nc.sync.dma_start(iw_sb[-1][:], iw.rearrange("(p t) j -> p t j", t=PACK))
+
+        load_iw(iw0, "s4_raw")
 
         pitch = 5 * J // 2
         late = sb("late", [P, PACK * pitch], F32)
@@ -100,7 +105,7 @@ def tile_list_dl_soft_geluP_kernel(
                 MULT,
             )
 
-        def weave_x(c):
+        def weave_all(c):
             nc.scalar.copy(
                 xg_bf[c].rearrange("p (g r i) -> p g i r", r=4, i=PACK),
                 picked[c].rearrange("p i (g r) -> p g i r", r=4),
@@ -144,9 +149,12 @@ def tile_list_dl_soft_geluP_kernel(
         for i in range(PACK - 1):
             for c in range(PICKS):
                 gather(c, i)
+            if i == 0:
+                load_iw(iw1, "x0")
             if i == 1:
+                load_iw(iw2, "x1")
                 weave_pair(0, 0)
-                weave_pair(1, 0)
+                weave_pair(2, 0)
         nc.scalar.copy(
             wd_bf.rearrange("p (t m i) -> p m i t", t=PACK, i=PACK),
             wd_sb[:].rearrange("p i (m t) -> p m i t", t=PACK),
@@ -154,88 +162,95 @@ def tile_list_dl_soft_geluP_kernel(
         gather(0, 3)
         gather(1, 3)
         weave_pair(0, 1)
-        weave_pair(1, 1)
+        weave_all(1)
         wd_codes = sb("wd_codes", [P, N], U32, tag="wgt1")
         nc.vector.quantize_mx(out=wd_codes[:].bitcast(FP8X4), scales=wd_sc[:], in_=wd_bf)
         quantize_x(0)
         gather(2, 3)
-        weave_x(2)
+        weave_pair(2, 1)
 
         def bank(index):
             return psum.tile([P, 512], F32, name="bank%d" % index)
 
+        blocks = J // JB
         pooled0 = [sb("pooled0_%d" % t, [P, J], F32) for t in range(PACK)]
-        pooled1 = [sb("pooled1_%d" % t, [P, J], F32) for t in range(PACK)]
-        partial = sb("partial", [P, PACK, J], F32)
+        biased0 = sb("biased0", [P, PACK, J], F32)
         acc0 = [bank(t) for t in range(PACK)]
         for t in range(PACK):
             project(acc0[t][:], 0, t, 0, J)
-        quantize_x(1)
-        acc1 = [bank(PACK + t) for t in range(PACK)]
-        for t in range(PACK):
-            project(acc1[t][:], 1, t, 0, J)
         for t in range(PACK):
             nc.vector.tensor_tensor(pooled0[t][:], acc0[t][:], iw_sb[0][:, t, :], MULT)
-        quantize_x(2)
-        for t in range(PACK):
-            nc.vector.tensor_tensor(pooled1[t][:], acc1[t][:], iw_sb[1][:, t, :], MULT)
-        for t in range(PACK):
-            nc.vector.scalar_tensor_tensor(
-                partial[:, t, :], pooled0[t][:], bias[:, t : t + 1], pooled1[t][:], ADD, ADD
-            )
+            nc.scalar.activation(biased0[:, t, :], pooled0[t][:], IDENTITY, bias=bias[:, t : t + 1])
+            if t == 0:
+                quantize_x(1)
+            if t == 2:
+                quantize_x(2)
 
         y_sc = sb("y_sc", [P, J], U8)
+        y_codes = sb("y_codes", [P, J], U32)
+        y_bf = sb("y_bf", [P, J * PACK], BF16)
         y_rows = out_0.rearrange("(p t) j -> p t j", t=PACK)
         y_words = out_1[0].rearrange("p j i -> p (j i)").bitcast(I32)
-        blocks = J // JB
-        acc2 = [bank(u) for u in range(blocks)]
-        pooled2 = [sb("pooled2_%d" % u, [P, PACK, JB], F32) for u in range(blocks)]
-        pieces = [(u * JB, JB) for u in range(blocks - 1)] + [(J - JB, JB // 2), (J - JB // 2, JB // 2)]
-        total = [sb("total%d" % v, [P, PACK, w], F32) for v, (j0, w) in enumerate(pieces)]
-        y_f32 = [sb("y_f32_%d" % v, [P, PACK, w], F32) for v, (j0, w) in enumerate(pieces)]
-        y_bf = [sb("y_bf%d" % v, [P, w * PACK], BF16) for v, (j0, w) in enumerate(pieces)]
-        y_codes = sb("y_codes", [P, J], U32)
+        pooled = {}
+        two = {}
 
-        def pool_last(u):
-            js = slice(u * JB, (u + 1) * JB)
+        def pool(c, u):
+            acc = bank(u if c == 2 else PACK + u)
+            for t in range(PACK):
+                project(acc[:, t * JB : (t + 1) * JB], c, t, u * JB, JB)
+            pooled[c, u] = sb("pooled%d_%d" % (c, u), [P, PACK, JB], F32)
             nc.vector.tensor_tensor(
-                pooled2[u][:], acc2[u][:].rearrange("p (t j) -> p t j", t=PACK), iw_sb[2][:, :, js], MULT
+                pooled[c, u][:],
+                acc[:].rearrange("p (t j) -> p t j", t=PACK),
+                iw_sb[c][:, :, u * JB : (u + 1) * JB],
+                MULT,
             )
 
-        def finish(v):
-            j0, w = pieces[v]
-            js = slice(j0, j0 + w)
-            nc.vector.tensor_tensor(
-                total[v][:], pooled2[j0 // JB][:, :, j0 % JB : j0 % JB + w], partial[:, :, js], ADD
-            )
+        def add_two(engine, u, tag=None):
+            two[u] = sb("two%d" % u, [P, PACK, JB], F32, tag=tag)
+            engine.tensor_tensor(two[u][:], biased0[:, :, u * JB : (u + 1) * JB], pooled[1, u][:], ADD)
+
+        def finish(engine, j0, w):
+            u, lo = divmod(j0, JB)
+            total = sb("total%d" % j0, [P, PACK, w], F32)
+            y_f32 = sb("y_f32_%d" % j0, [P, PACK, w], F32)
+            engine.tensor_tensor(total[:], two[u][:, :, lo : lo + w], pooled[2, u][:, :, lo : lo + w], ADD)
             nc.scalar.activation(
-                y_bf[v][:].rearrange("p (g r t) -> p g t r", r=4, t=PACK),
-                total[v][:].rearrange("p t (g r) -> p g t r", r=4),
+                y_bf[:, j0 * PACK : (j0 + w) * PACK].rearrange("p (g r t) -> p g t r", r=4, t=PACK),
+                total[:].rearrange("p t (g r) -> p g t r", r=4),
                 GELU,
             )
-            nc.scalar.activation(y_f32[v][:], total[v][:], GELU)
-            nc.sync.dma_start(y_rows[:, :, js], y_f32[v][:])
+            nc.scalar.activation(y_f32[:], total[:], GELU)
+            nc.sync.dma_start(y_rows[:, :, j0 : j0 + w], y_f32[:])
 
-        def hand_on(v):
-            j0, w = pieces[v]
-            js = slice(j0, j0 + w)
-            nc.vector.quantize_mx(out=y_codes[:, js].bitcast(FP8X4), scales=y_sc[:, js], in_=y_bf[v][:])
-            if j0 + w == J - JB:
-                nc.sync.dma_start(y_words[:, 0 : J - JB], y_codes[:, 0 : J - JB].bitcast(I32))
-            if j0 + w == J:
-                nc.sync.dma_start(y_words[:, J - JB : J], y_codes[:, J - JB : J].bitcast(I32))
+        def hand_on(j0, w):
+            nc.vector.quantize_mx(
+                out=y_codes[:, j0 : j0 + w].bitcast(FP8X4),
+                scales=y_sc[:, j0 : j0 + w],
+                in_=y_bf[:, j0 * PACK : (j0 + w) * PACK],
+            )
+
+        def store_words(j0, w):
+            nc.sync.dma_start(y_words[:, j0 : j0 + w], y_codes[:, j0 : j0 + w].bitcast(I32))
 
         for u in range(blocks):
-            for t in range(PACK):
-                project(acc2[u][:, t * JB : (t + 1) * JB], 2, t, u * JB, JB)
-        pool_last(0)
-        for v in range(len(pieces)):
-            if v + 1 < blocks:
-                pool_last(v + 1)
-            finish(v)
-            if v >= 1:
-                hand_on(v - 1)
-        hand_on(len(pieces) - 1)
+            pool(1, u)
+            pool(2, u)
+        add_two(nc.gpsimd, 0)
+        finish(nc.gpsimd, 0, JB)
+        add_two(nc.vector, 1, tag="pooled2_0")
+        finish(nc.vector, JB, JB)
+        add_two(nc.vector, 2, tag="pooled1_1")
+        finish(nc.vector, 2 * JB, JB)
+        add_two(nc.vector, 3, tag="pooled1_2")
+        hand_on(0, 2 * JB)
+        finish(nc.vector, 3 * JB, JB // 2)
+        finish(nc.vector, 3 * JB + JB // 2, JB // 2)
+        hand_on(2 * JB, JB)
+        store_words(0, 3 * JB)
+        hand_on(3 * JB, JB // 2)
+        hand_on(3 * JB + JB // 2, JB // 2)
+        store_words(3 * JB, JB)
         for q in range(4):
             queue = nc.scalar if q % 2 else nc.sync
             queue.dma_start(out_2[0, 4 * q : 4 * q + 4, :].bitcast(I32), y_sc[32 * q : 32 * q + 4, :].bitcast(I32))

@@ -43,18 +43,19 @@ def tile_list_dl_soft_geluP_kernel(
         s4_raw = sb("s4_raw", [P, N], U8)
         bias = sb("bias", [P, PACK], F32)
 
-        def load_wgt(c):
-            nc.sync.dma_start(wgt_sb[c][:], wgt[:, c * J : (c + 1) * J])
+        def load_wgt(c, lo=0, hi=J):
+            nc.sync.dma_start(wgt_sb[c][:, lo:hi], wgt[:, c * J + lo : c * J + hi])
 
         def load_x(i):
             nc.sync.dma_start(x_sb[i][:], x_rows[i])
 
         nc.vector.memset(s4_raw[:].bitcast(I32), 0)
         nc.sync.dma_start(offsets[:], offs)
-        load_wgt(0)
+        load_wgt(0, 0, JB)
         load_x(0)
         nc.scalar.dma_start(w4_raw[:].bitcast(I32), w4_words[0].bitcast(I32))
         nc.scalar.dma_start(s4_raw[0:16, :].bitcast(I32), w4_scales[0].bitcast(I32))
+        load_wgt(0, JB, J)
         load_wgt(1)
         load_wgt(2)
         load_x(1)
@@ -96,12 +97,11 @@ def tile_list_dl_soft_geluP_kernel(
         wd_bf = late[:, seam : seam + 2 * J].bitcast(BF16)
         wd_sc = sb("wd_sc", [P, N], U8)
 
-        def gather(c, i):
-            cols = J // 16
+        def gather(c, i, lo=0, hi=J):
             nc.vector.tensor_tensor(
-                picked[c][:, i, :],
-                x_sb[i][:].indirect(offsets[:, c * cols : (c + 1) * cols]),
-                wgt_sb[c][:],
+                picked[c][:, i, lo:hi],
+                x_sb[i][:].indirect(offsets[:, (c * J + lo) // 16 : (c * J + hi) // 16]),
+                wgt_sb[c][:, lo:hi],
                 MULT,
             )
 
@@ -148,7 +148,11 @@ def tile_list_dl_soft_geluP_kernel(
 
         for i in range(PACK - 1):
             for c in range(PICKS):
-                gather(c, i)
+                if i == 0 and c == 0:
+                    gather(c, i, 0, JB)
+                    gather(c, i, JB, J)
+                else:
+                    gather(c, i)
             if i == 0:
                 load_iw(iw1, "x0")
             if i == 1:
@@ -163,7 +167,7 @@ def tile_list_dl_soft_geluP_kernel(
         gather(1, 3)
         weave_pair(0, 1)
         weave_all(1)
-        wd_codes = sb("wd_codes", [P, N], U32, tag="wgt1")
+        wd_codes = sb("wd_codes", [P, N], U32, tag="wgt0")
         nc.vector.quantize_mx(out=wd_codes[:].bitcast(FP8X4), scales=wd_sc[:], in_=wd_bf)
         quantize_x(0)
         gather(2, 3)
@@ -194,34 +198,40 @@ def tile_list_dl_soft_geluP_kernel(
         pooled = {}
         two = {}
 
-        def pool(c, u):
-            acc = bank(u if c == 2 else PACK + u)
+        def block(tile, u):
+            return tile[:, :, u * JB : (u + 1) * JB]
+
+        def fresh(name):
+            return sb(name, [P, PACK, JB], F32)[:]
+
+        def pool(c, u, bank_index, into):
+            acc = bank(bank_index)
             for t in range(PACK):
                 project(acc[:, t * JB : (t + 1) * JB], c, t, u * JB, JB)
-            pooled[c, u] = sb("pooled%d_%d" % (c, u), [P, PACK, JB], F32)
-            nc.vector.tensor_tensor(
-                pooled[c, u][:],
-                acc[:].rearrange("p (t j) -> p t j", t=PACK),
-                iw_sb[c][:, :, u * JB : (u + 1) * JB],
-                MULT,
+            pooled[c, u] = into
+            nc.vector.tensor_tensor(into, acc[:].rearrange("p (t j) -> p t j", t=PACK), block(iw_sb[c], u), MULT)
+
+        def add_two(engine, u, into):
+            two[u] = into
+            engine.tensor_tensor(two[u], biased0[:, :, u * JB : (u + 1) * JB], pooled[1, u], ADD)
+
+        total = [sb("total%d" % u, [P, PACK, JB], F32) for u in range(blocks)]
+
+        def add_three(engine, u, lo, w):
+            j0 = u * JB + lo
+            engine.tensor_tensor(
+                total[u][:, :, lo : lo + w], two[u][:, :, lo : lo + w], pooled[2, u][:, :, lo : lo + w], ADD
             )
-
-        def add_two(engine, u, tag=None):
-            two[u] = sb("two%d" % u, [P, PACK, JB], F32, tag=tag)
-            engine.tensor_tensor(two[u][:], biased0[:, :, u * JB : (u + 1) * JB], pooled[1, u][:], ADD)
-
-        def finish(engine, j0, w):
-            u, lo = divmod(j0, JB)
-            total = sb("total%d" % j0, [P, PACK, w], F32)
-            y_f32 = sb("y_f32_%d" % j0, [P, PACK, w], F32)
-            engine.tensor_tensor(total[:], two[u][:, :, lo : lo + w], pooled[2, u][:, :, lo : lo + w], ADD)
             nc.scalar.activation(
                 y_bf[:, j0 * PACK : (j0 + w) * PACK].rearrange("p (g r t) -> p g t r", r=4, t=PACK),
-                total[:].rearrange("p t (g r) -> p g t r", r=4),
+                total[u][:, :, lo : lo + w].rearrange("p t (g r) -> p g t r", r=4),
                 GELU,
             )
-            nc.scalar.activation(y_f32[:], total[:], GELU)
-            nc.sync.dma_start(y_rows[:, :, j0 : j0 + w], y_f32[:])
+
+        def store_rows(u):
+            y_f32 = sb("y_f32_%d" % u, [P, PACK, JB], F32)
+            nc.scalar.activation(y_f32[:], total[u][:], GELU)
+            nc.sync.dma_start(y_rows[:, :, u * JB : (u + 1) * JB], y_f32[:])
 
         def hand_on(j0, w):
             nc.vector.quantize_mx(
@@ -233,19 +243,29 @@ def tile_list_dl_soft_geluP_kernel(
         def store_words(j0, w):
             nc.sync.dma_start(y_words[:, j0 : j0 + w], y_codes[:, j0 : j0 + w].bitcast(I32))
 
-        for u in range(blocks):
-            pool(1, u)
-            pool(2, u)
-        add_two(nc.gpsimd, 0)
-        finish(nc.gpsimd, 0, JB)
-        add_two(nc.vector, 1, tag="pooled2_0")
-        finish(nc.vector, JB, JB)
-        add_two(nc.vector, 2, tag="pooled1_1")
-        finish(nc.vector, 2 * JB, JB)
-        add_two(nc.vector, 3, tag="pooled1_2")
+        last = blocks - 1
+        pool(1, 0, 4, fresh("pooled1_0"))
+        pool(2, 0, 0, fresh("pooled2_0"))
+        pool(1, 1, 5, fresh("pooled1_1"))
+        pool(2, 1, 1, fresh("pooled2_1"))
+        pool(1, 2, 6, block(iw_sb[2], 0))
+        pool(2, 2, 2, fresh("pooled2_2"))
+        pool(1, 3, 7, block(iw_sb[2], 1))
+        add_two(nc.gpsimd, 0, fresh("two0"))
+        add_three(nc.gpsimd, 0, 0, JB)
+        store_rows(0)
+        add_two(nc.vector, 1, block(iw_sb[2], 2))
+        add_two(nc.vector, 2, block(iw_sb[1], 3))
+        add_three(nc.vector, 1, 0, JB)
+        store_rows(1)
+        add_two(nc.vector, 3, pooled[1, 1])
+        add_three(nc.vector, 2, 0, JB)
+        store_rows(2)
+        pool(2, last, 3, pooled[2, 1])
         hand_on(0, 2 * JB)
-        finish(nc.vector, 3 * JB, JB // 2)
-        finish(nc.vector, 3 * JB + JB // 2, JB // 2)
+        add_three(nc.vector, last, 0, JB // 2)
+        add_three(nc.vector, last, JB // 2, JB // 2)
+        store_rows(last)
         hand_on(2 * JB, JB)
         store_words(0, 3 * JB)
         hand_on(3 * JB, JB // 2)

@@ -66,8 +66,8 @@ def tile_list_dl_soft_geluP_kernel(
         w4_codes = sb("w4_codes", [P, 2 * N], U8)
         w4_sc = sb("w4_sc", [P, N], U8)
         nc.vector.tensor_copy(
-            w4_codes[:].rearrange("p (t m e) -> p t m e", t=PACK, e=2),
-            w4_raw[:].rearrange("p (m t e) -> p t m e", t=PACK, e=2),
+            w4_codes[:].bitcast(U16).rearrange("p (t m) -> p t m", t=PACK),
+            w4_raw[:].bitcast(U16).rearrange("p (m t) -> p t m", t=PACK),
         )
         nc.vector.tensor_copy(
             w4_sc[:].rearrange("p (t m) -> p t m", t=PACK),
@@ -184,11 +184,13 @@ def tile_list_dl_soft_geluP_kernel(
             project(acc0[t][:], 0, t, 0, J)
         for t in range(PACK):
             nc.vector.tensor_tensor(pooled0[t][:], acc0[t][:], iw_sb[0][:, t, :], MULT)
-            nc.scalar.activation(biased0[:, t, :], pooled0[t][:], IDENTITY, bias=bias[:, t : t + 1])
-            if t == 0:
+            nc.scalar.activation(biased0[:, t, 0:JB], pooled0[t][:, 0:JB], IDENTITY, bias=bias[:, t : t + 1])
+            if t == 1:
                 quantize_x(1)
             if t == 2:
                 quantize_x(2)
+        for t in range(PACK):
+            nc.scalar.activation(biased0[:, t, JB:J], pooled0[t][:, JB:J], IDENTITY, bias=bias[:, t : t + 1])
 
         y_sc = sb("y_sc", [P, J], U8)
         y_codes = sb("y_codes", [P, J], U32)

@@ -49,12 +49,12 @@ def tile_list_dl_soft_geluP_kernel(
         def load_x(i):
             nc.sync.dma_start(x_sb[i][:], x_rows[i])
 
-        nc.vector.memset(s4_raw[:].bitcast(I32), 0)
+        nc.gpsimd.memset(s4_raw[:].bitcast(I32), 0)
         nc.sync.dma_start(offsets[:], offs)
-        load_wgt(0, 0, JB)
-        load_x(0)
         nc.scalar.dma_start(w4_raw[:].bitcast(I32), w4_words[0].bitcast(I32))
         nc.scalar.dma_start(s4_raw[0:16, :].bitcast(I32), w4_scales[0].bitcast(I32))
+        load_wgt(0, 0, JB)
+        load_x(0)
         load_wgt(0, JB, J)
         load_wgt(1)
         load_wgt(2)
@@ -77,44 +77,52 @@ def tile_list_dl_soft_geluP_kernel(
         for q in range(1, 4):
             nc.sync.dma_start(w4_sc[32 * q : 32 * q + 4, :].bitcast(I32), w4_sc[4 * q : 4 * q + 4, :].bitcast(I32))
         nc.sync.dma_start(bias[:], b.rearrange("(p t) -> p t", t=PACK))
-        iw_sb = []
+        iw_sb = {}
 
-        def load_iw(iw, after):
-            iw_sb.append(sb("iw%d" % len(iw_sb), [P, PACK, J], F32, tag=after))
-            nc.sync.dma_start(iw_sb[-1][:], iw.rearrange("(p t) j -> p t j", t=PACK))
+        def load_iw(c, h, after):
+            iw_sb[c, h] = sb("iw%d_%d" % (c, h), [P, PACK, J // 2], F32, tag=after)
+            rows = (iw0, iw1, iw2)[c].rearrange("(p t) j -> p t j", t=PACK)
+            nc.sync.dma_start(iw_sb[c, h][:], rows[:, :, h * J // 2 : (h + 1) * J // 2])
 
-        load_iw(iw0, "s4_raw")
+        load_iw(0, 0, "s4_raw")
+        load_iw(1, 0, "w4_raw")
 
-        pitch = 5 * J // 2
-        late = sb("late", [P, PACK * pitch], F32)
-        picked = [sb("picked%d" % c, [P, PACK, J], F32)[:] for c in range(PICKS - 1)]
-        picked.append(late[:].rearrange("p (i w) -> p i w", i=PACK)[:, :, 0:J])
-        seam = 3 * pitch + J // 2
-        xg_bf = [late[:, seam - 2 * J : seam].bitcast(BF16)]
-        xg_bf.extend(sb("xg_bf%d" % c, [P, J * PACK], BF16)[:] for c in range(1, PICKS))
+        late = sb("late", [P, 5 * J], F32)
+        lo0 = sb("lo0", [P, 2, J], F32)
+        lo1 = sb("lo1", [P, 2, J], F32)
+        hi1 = sb("hi1", [P, 2, J], F32)
+        pairs = {
+            (0, 0): lo0[:],
+            (0, 1): late[:, 3 * J : 5 * J].rearrange("p (e j) -> p e j", e=2),
+            (1, 0): lo1[:],
+            (1, 1): hi1[:],
+        }
+        planes2 = late[:, 0 : 4 * J].rearrange("p (i j) -> p i j", i=PACK)
+        xg_bf = [sb("xg_bf%d" % c, [P, J * PACK], BF16)[:] for c in range(PICKS)]
         xg_codes = [sb("xg_codes%d" % c, [P, J], U32) for c in range(PICKS)]
         xg_sc = [sb("xg_sc%d" % c, [P, J], U8) for c in range(PICKS)]
-        wd_bf = late[:, seam : seam + 2 * J].bitcast(BF16)
+        wd_bf = sb("wd_bf", [P, N * PACK], BF16)[:]
         wd_sc = sb("wd_sc", [P, N], U8)
 
         def gather(c, i, lo=0, hi=J):
+            into = planes2[:, i, lo:hi] if c == 2 else pairs[c, i // 2][:, i % 2, lo:hi]
             nc.vector.tensor_tensor(
-                picked[c][:, i, lo:hi],
+                into,
                 x_sb[i][:].indirect(offsets[:, (c * J + lo) // 16 : (c * J + hi) // 16]),
                 wgt_sb[c][:, lo:hi],
                 MULT,
             )
 
-        def weave_all(c):
+        def weave_all():
             nc.scalar.copy(
-                xg_bf[c].rearrange("p (g r i) -> p g i r", r=4, i=PACK),
-                picked[c].rearrange("p i (g r) -> p g i r", r=4),
+                xg_bf[2].rearrange("p (g r i) -> p g i r", r=4, i=PACK),
+                planes2.rearrange("p i (g r) -> p g i r", r=4),
             )
 
         def weave_pair(c, u):
             nc.scalar.copy(
                 xg_bf[c].rearrange("p (j u e) -> p u j e", u=2, e=2)[:, u],
-                picked[c][:, 2 * u : 2 * u + 2, :].rearrange("p e j -> p j e"),
+                pairs[c, u].rearrange("p e j -> p j e"),
             )
 
         def quantize_x(c):
@@ -154,11 +162,13 @@ def tile_list_dl_soft_geluP_kernel(
                 else:
                     gather(c, i)
             if i == 0:
-                load_iw(iw1, "x0")
+                load_iw(2, 0, "x0")
             if i == 1:
-                load_iw(iw2, "x1")
+                load_iw(0, 1, "x1")
                 weave_pair(0, 0)
-                weave_pair(2, 0)
+                weave_pair(1, 0)
+                load_iw(1, 1, "lo0")
+                load_iw(2, 1, "lo1")
         nc.scalar.copy(
             wd_bf.rearrange("p (t m i) -> p m i t", t=PACK, i=PACK),
             wd_sb[:].rearrange("p i (m t) -> p m i t", t=PACK),
@@ -166,31 +176,13 @@ def tile_list_dl_soft_geluP_kernel(
         gather(0, 3)
         gather(1, 3)
         weave_pair(0, 1)
-        weave_all(1)
+        weave_pair(1, 1)
         wd_codes = sb("wd_codes", [P, N], U32, tag="wgt0")
         nc.vector.quantize_mx(out=wd_codes[:].bitcast(FP8X4), scales=wd_sc[:], in_=wd_bf)
         quantize_x(0)
         gather(2, 3)
-        weave_pair(2, 1)
-
-        def bank(index):
-            return psum.tile([P, 512], F32, name="bank%d" % index)
-
-        blocks = J // JB
-        pooled0 = [sb("pooled0_%d" % t, [P, J], F32) for t in range(PACK)]
-        biased0 = sb("biased0", [P, PACK, J], F32)
-        acc0 = [bank(t) for t in range(PACK)]
-        for t in range(PACK):
-            project(acc0[t][:], 0, t, 0, J)
-        for t in range(PACK):
-            nc.vector.tensor_tensor(pooled0[t][:], acc0[t][:], iw_sb[0][:, t, :], MULT)
-            nc.scalar.activation(biased0[:, t, 0:JB], pooled0[t][:, 0:JB], IDENTITY, bias=bias[:, t : t + 1])
-            if t == 1:
-                quantize_x(1)
-            if t == 2:
-                quantize_x(2)
-        for t in range(PACK):
-            nc.scalar.activation(biased0[:, t, JB:J], pooled0[t][:, JB:J], IDENTITY, bias=bias[:, t : t + 1])
+        weave_all()
+        quantize_x(1)
 
         y_sc = sb("y_sc", [P, J], U8)
         y_codes = sb("y_codes", [P, J], U32)
@@ -199,25 +191,33 @@ def tile_list_dl_soft_geluP_kernel(
         y_words = out_1[0].rearrange("p j i -> p (j i)").bitcast(I32)
         pooled = {}
         two = {}
+        total = {}
+        banks = []
 
-        def block(tile, u):
-            return tile[:, :, u * JB : (u + 1) * JB]
+        def fresh(name, tag=None):
+            return sb(name, [P, PACK, JB], F32, tag=tag)[:]
 
-        def fresh(name):
-            return sb(name, [P, PACK, JB], F32)[:]
-
-        def pool(c, u, bank_index, into):
-            acc = bank(bank_index)
+        def pool(c, u, into=None):
+            acc = psum.tile([P, 512], F32, name="bank%d" % (len(banks) % 8))
+            banks.append(acc)
             for t in range(PACK):
                 project(acc[:, t * JB : (t + 1) * JB], c, t, u * JB, JB)
-            pooled[c, u] = into
-            nc.vector.tensor_tensor(into, acc[:].rearrange("p (t j) -> p t j", t=PACK), block(iw_sb[c], u), MULT)
+            pooled[c, u] = fresh("pooled%d_%d" % (c, u)) if into is None else into
+            nc.vector.tensor_tensor(
+                pooled[c, u],
+                acc[:].rearrange("p (t j) -> p t j", t=PACK),
+                iw_sb[c, u // 2][:, :, u % 2 * JB : (u % 2 + 1) * JB],
+                MULT,
+            )
+            if c == 0:
+                raw = pooled[c, u]
+                pooled[c, u] = fresh("biased%d" % u)
+                for t in range(PACK):
+                    nc.scalar.activation(pooled[c, u][:, t, :], raw[:, t, :], IDENTITY, bias=bias[:, t : t + 1])
 
         def add_two(engine, u, into):
             two[u] = into
-            engine.tensor_tensor(two[u], biased0[:, :, u * JB : (u + 1) * JB], pooled[1, u], ADD)
-
-        total = [sb("total%d" % u, [P, PACK, JB], F32) for u in range(blocks)]
+            engine.tensor_tensor(into, pooled[0, u], pooled[1, u], ADD)
 
         def add_three(engine, u, lo, w):
             j0 = u * JB + lo
@@ -232,7 +232,7 @@ def tile_list_dl_soft_geluP_kernel(
 
         def store_rows(u):
             y_f32 = sb("y_f32_%d" % u, [P, PACK, JB], F32)
-            nc.scalar.activation(y_f32[:], total[u][:], GELU)
+            nc.scalar.activation(y_f32[:], total[u], GELU)
             nc.sync.dma_start(y_rows[:, :, u * JB : (u + 1) * JB], y_f32[:])
 
         def hand_on(j0, w):
@@ -245,34 +245,43 @@ def tile_list_dl_soft_geluP_kernel(
         def store_words(j0, w):
             nc.sync.dma_start(y_words[:, j0 : j0 + w], y_codes[:, j0 : j0 + w].bitcast(I32))
 
-        last = blocks - 1
-        pool(1, 0, 4, fresh("pooled1_0"))
-        pool(2, 0, 0, fresh("pooled2_0"))
-        pool(1, 1, 5, fresh("pooled1_1"))
-        pool(2, 1, 1, fresh("pooled2_1"))
-        pool(1, 2, 6, block(iw_sb[2], 0))
-        pool(2, 2, 2, fresh("pooled2_2"))
-        pool(1, 3, 7, block(iw_sb[2], 1))
-        add_two(nc.gpsimd, 0, fresh("two0"))
+        first = sb("first", [P, 2, PACK, JB], F32, tag="hi1")
+        pool(0, 0, first[:, 0])
+        pool(0, 1, first[:, 1])
+        pool(1, 0)
+        quantize_x(2)
+        for u in (0, 2, 3):
+            total[u] = fresh("total%d" % u)
+        second = sb("second", [P, 3, PACK, JB], F32, tag="late")
+        add_two(nc.gpsimd, 0, fresh("two0", tag="xg_bf2"))
+        pool(1, 1, second[:, 2])
+        pool(0, 2, second[:, 0])
+        pool(2, 0)
         add_three(nc.gpsimd, 0, 0, JB)
         store_rows(0)
-        add_two(nc.vector, 1, block(iw_sb[2], 2))
-        add_two(nc.vector, 2, block(iw_sb[1], 3))
+        add_two(nc.gpsimd, 1, fresh("two1", tag="biased0"))
+        pool(2, 1)
+        pool(1, 2)
+        pool(2, 2)
+        pool(0, 3, second[:, 1])
+        total[1] = fresh("total1", tag="pooled2_0")
         add_three(nc.vector, 1, 0, JB)
         store_rows(1)
-        add_two(nc.vector, 3, pooled[1, 1])
+        pool(1, 3)
+        add_two(nc.vector, 2, second[:, 2])
+        pool(2, 3)
         add_three(nc.vector, 2, 0, JB)
         store_rows(2)
-        pool(2, last, 3, pooled[2, 1])
+        add_two(nc.vector, 3, fresh("two3", tag="biased1"))
         hand_on(0, 2 * JB)
-        add_three(nc.vector, last, 0, JB // 2)
-        add_three(nc.vector, last, JB // 2, JB // 2)
-        store_rows(last)
+        store_words(0, 2 * JB)
+        add_three(nc.vector, 3, 0, JB // 2)
+        add_three(nc.vector, 3, JB // 2, JB // 2)
+        store_rows(3)
         hand_on(2 * JB, JB)
-        store_words(0, 3 * JB)
         hand_on(3 * JB, JB // 2)
         hand_on(3 * JB + JB // 2, JB // 2)
-        store_words(3 * JB, JB)
+        store_words(2 * JB, 2 * JB)
         for q in range(4):
             queue = nc.scalar if q % 2 else nc.sync
             queue.dma_start(out_2[0, 4 * q : 4 * q + 4, :].bitcast(I32), y_sc[32 * q : 32 * q + 4, :].bitcast(I32))

@@ -19,7 +19,6 @@ FP8X4 = mybir.dt.float8_e4m3fn_x4
 FP4X4 = mybir.dt.float4_e2m1fn_x4
 MULT = mybir.AluOpType.mult
 ADD = mybir.AluOpType.add
-IDENTITY = mybir.ActivationFunctionType.Identity
 GELU = mybir.ActivationFunctionType.Gelu_apprx_tanh
 
 
@@ -37,7 +36,8 @@ def tile_list_dl_soft_geluP_kernel(
         offsets = keep.tile([P, PICKS * J // 16], U16, name="offsets")
         x_rows = xT.rearrange("(p i) t -> i p t", i=PACK)
         x_sb = [sb("x%d" % i, [P, T], F32) for i in range(PACK)]
-        wgt_sb = [sb("wgt%d" % c, [P, J], F32) for c in range(PICKS)]
+        late = sb("late", [P, 6 * J], F32)
+        wgt_sb = [late[:, 2 * J : 3 * J]] + [sb("wgt%d" % c, [P, J], F32)[:] for c in range(1, PICKS)]
         wd_sb = sb("wd", [P, PACK, N], F32)
         w4_raw = sb("w4_raw", [P, 2 * N], U8)
         s4_raw = sb("s4_raw", [P, N], U8)
@@ -60,8 +60,8 @@ def tile_list_dl_soft_geluP_kernel(
         load_wgt(2)
         load_x(1)
         load_x(2)
-        nc.sync.dma_start(wd_sb[:], wd.rearrange("(p i) n -> p i n", i=PACK))
         load_x(3)
+        nc.sync.dma_start(wd_sb[:], wd.rearrange("(p i) n -> p i n", i=PACK))
 
         w4_codes = sb("w4_codes", [P, 2 * N], U8)
         w4_sc = sb("w4_sc", [P, N], U8)
@@ -87,15 +87,13 @@ def tile_list_dl_soft_geluP_kernel(
         load_iw(0, 0, "s4_raw")
         load_iw(1, 0, "w4_raw")
 
-        late = sb("late", [P, 5 * J], F32)
         lo0 = sb("lo0", [P, 2, J], F32)
         lo1 = sb("lo1", [P, 2, J], F32)
-        hi1 = sb("hi1", [P, 2, J], F32)
         pairs = {
             (0, 0): lo0[:],
             (0, 1): late[:, 3 * J : 5 * J].rearrange("p (e j) -> p e j", e=2),
             (1, 0): lo1[:],
-            (1, 1): hi1[:],
+            (1, 1): late[:, 4 * J : 6 * J].rearrange("p (e j) -> p e j", e=2),
         }
         planes2 = late[:, 0 : 4 * J].rearrange("p (i j) -> p i j", i=PACK)
         xg_bf = [sb("xg_bf%d" % c, [P, J * PACK], BF16)[:] for c in range(PICKS)]
@@ -128,18 +126,18 @@ def tile_list_dl_soft_geluP_kernel(
         def quantize_x(c):
             nc.vector.quantize_mx(out=xg_codes[c][:].bitcast(FP8X4), scales=xg_sc[c][:], in_=xg_bf[c])
 
-        def base_pass(out, c, t, j0, width):
+        def base_pass(out, c, t, j0, width, start=True):
             nc.tensor.matmul_mx(
                 out=out,
                 lhsT=w4_codes[:, 2 * P * t : 2 * P * (t + 1)].bitcast(FP4X4),
                 lhsT_scale=w4_sc[:, P * t : P * (t + 1)],
                 rhs=xg_codes[c][:, j0 : j0 + width].bitcast(FP8X4),
                 rhs_scale=xg_sc[c][:, j0 : j0 + width],
-                start=True,
+                start=start,
                 stop=False,
             )
 
-        def delta_pass(out, c, t, j0, width):
+        def delta_pass(out, c, t, j0, width, stop=True):
             nc.tensor.matmul_mx(
                 out=out,
                 lhsT=wd_codes[:, P * t : P * (t + 1)].bitcast(FP8X4),
@@ -147,14 +145,14 @@ def tile_list_dl_soft_geluP_kernel(
                 rhs=xg_codes[c][:, j0 : j0 + width].bitcast(FP8X4),
                 rhs_scale=xg_sc[c][:, j0 : j0 + width],
                 start=False,
-                stop=True,
+                stop=stop,
             )
 
         def project(out, c, t, j0, width):
             base_pass(out, c, t, j0, width)
             delta_pass(out, c, t, j0, width)
 
-        for i in range(PACK - 1):
+        for i in range(2):
             for c in range(PICKS):
                 if i == 0 and c == 0:
                     gather(c, i, 0, JB)
@@ -163,23 +161,25 @@ def tile_list_dl_soft_geluP_kernel(
                     gather(c, i)
             if i == 0:
                 load_iw(2, 0, "x0")
-            if i == 1:
-                load_iw(0, 1, "x1")
-                weave_pair(0, 0)
-                weave_pair(1, 0)
-                load_iw(1, 1, "lo0")
-                load_iw(2, 1, "lo1")
+        load_iw(0, 1, "x1")
+        weave_pair(0, 0)
+        weave_pair(1, 0)
+        load_iw(1, 1, "lo0")
+        load_iw(2, 1, "lo1")
+        gather(0, 2)
+        gather(0, 3)
+        weave_pair(0, 1)
+        gather(1, 3)
+        gather(2, 2)
+        quantize_x(0)
         nc.scalar.copy(
             wd_bf.rearrange("p (t m i) -> p m i t", t=PACK, i=PACK),
             wd_sb[:].rearrange("p i (m t) -> p m i t", t=PACK),
         )
-        gather(0, 3)
-        gather(1, 3)
-        weave_pair(0, 1)
+        gather(1, 2)
         weave_pair(1, 1)
-        wd_codes = sb("wd_codes", [P, N], U32, tag="wgt0")
+        wd_codes = sb("wd_codes", [P, N], U32)
         nc.vector.quantize_mx(out=wd_codes[:].bitcast(FP8X4), scales=wd_sc[:], in_=wd_bf)
-        quantize_x(0)
         gather(2, 3)
         weave_all()
         quantize_x(1)
@@ -192,16 +192,25 @@ def tile_list_dl_soft_geluP_kernel(
         pooled = {}
         two = {}
         total = {}
-        banks = []
+        bank_of = ((4, 5, 1, 4), (6, 7, 0, 5))
+        early = [psum.tile([P, 512], F32, name="bank%d" % u) for u in range(4)]
+        for u in range(4):
+            for t in range(PACK):
+                base_pass(early[u][:, t * JB : (t + 1) * JB], 0, t, u * JB, JB, start=t == 0)
+        for u in range(4):
+            for t in range(PACK):
+                delta_pass(early[u][:, t * JB : (t + 1) * JB], 0, t, u * JB, JB, stop=t == PACK - 1)
 
         def fresh(name, tag=None):
             return sb(name, [P, PACK, JB], F32, tag=tag)[:]
 
         def pool(c, u, into=None):
-            acc = psum.tile([P, 512], F32, name="bank%d" % (len(banks) % 8))
-            banks.append(acc)
-            for t in range(PACK):
-                project(acc[:, t * JB : (t + 1) * JB], c, t, u * JB, JB)
+            if c == 0:
+                acc = early[u]
+            else:
+                acc = psum.tile([P, 512], F32, name="bank%d" % bank_of[c - 1][u])
+                for t in range(PACK):
+                    project(acc[:, t * JB : (t + 1) * JB], c, t, u * JB, JB)
             pooled[c, u] = fresh("pooled%d_%d" % (c, u)) if into is None else into
             nc.vector.tensor_tensor(
                 pooled[c, u],
@@ -209,15 +218,28 @@ def tile_list_dl_soft_geluP_kernel(
                 iw_sb[c, u // 2][:, :, u % 2 * JB : (u % 2 + 1) * JB],
                 MULT,
             )
-            if c == 0:
-                raw = pooled[c, u]
-                pooled[c, u] = fresh("biased%d" % u)
-                for t in range(PACK):
-                    nc.scalar.activation(pooled[c, u][:, t, :], raw[:, t, :], IDENTITY, bias=bias[:, t : t + 1])
 
         def add_two(engine, u, into):
             two[u] = into
             engine.tensor_tensor(into, pooled[0, u], pooled[1, u], ADD)
+
+        def add_two_biased(u, into, slices):
+            two[u] = into
+            for t in slices:
+                nc.vector.scalar_tensor_tensor(
+                    into[:, t, :], pooled[0, u][:, t, :], bias[:, t : t + 1], pooled[1, u][:, t, :], ADD, ADD
+                )
+
+        def finish_unbiased(engine, u):
+            engine.tensor_tensor(total[u], two[u], pooled[2, u], ADD)
+            y_f32 = sb("y_f32_%d" % u, [P, PACK, JB], F32)
+            for t in range(PACK):
+                nc.scalar.activation(y_f32[:, t, :], total[u][:, t, :], GELU, bias=bias[:, t : t + 1])
+            nc.sync.dma_start(y_rows[:, :, u * JB : (u + 1) * JB], y_f32[:])
+            nc.scalar.copy(
+                y_bf[:, u * JB * PACK : (u + 1) * JB * PACK].rearrange("p (g r t) -> p g t r", r=4, t=PACK),
+                y_f32[:].rearrange("p t (g r) -> p g t r", r=4),
+            )
 
         def add_three(engine, u, lo, w):
             j0 = u * JB + lo
@@ -245,34 +267,33 @@ def tile_list_dl_soft_geluP_kernel(
         def store_words(j0, w):
             nc.sync.dma_start(y_words[:, j0 : j0 + w], y_codes[:, j0 : j0 + w].bitcast(I32))
 
-        first = sb("first", [P, 2, PACK, JB], F32, tag="hi1")
+        first = late[:, 4 * J : 6 * J].rearrange("p (u t j) -> p u t j", u=2, t=PACK)
         pool(0, 0, first[:, 0])
         pool(0, 1, first[:, 1])
         pool(1, 0)
         quantize_x(2)
         for u in (0, 2, 3):
             total[u] = fresh("total%d" % u)
-        second = sb("second", [P, 3, PACK, JB], F32, tag="late")
+        second = late[:, 0 : 3 * J].rearrange("p (u t j) -> p u t j", u=3, t=PACK)
         add_two(nc.gpsimd, 0, fresh("two0", tag="xg_bf2"))
         pool(1, 1, second[:, 2])
         pool(0, 2, second[:, 0])
         pool(2, 0)
-        add_three(nc.gpsimd, 0, 0, JB)
-        store_rows(0)
-        add_two(nc.gpsimd, 1, fresh("two1", tag="biased0"))
+        finish_unbiased(nc.gpsimd, 0)
         pool(2, 1)
         pool(1, 2)
-        pool(2, 2)
+        add_two(nc.gpsimd, 1, iw_sb[1, 1][:, :, 0:JB])
         pool(0, 3, second[:, 1])
-        total[1] = fresh("total1", tag="pooled2_0")
-        add_three(nc.vector, 1, 0, JB)
-        store_rows(1)
+        pool(2, 2)
         pool(1, 3)
-        add_two(nc.vector, 2, second[:, 2])
         pool(2, 3)
+        total[1] = iw_sb[1, 1][:, :, JB : 2 * JB]
+        finish_unbiased(nc.vector, 1)
+        add_two_biased(2, second[:, 2], range(PACK))
+        add_two_biased(3, second[:, 0], (0, 1))
         add_three(nc.vector, 2, 0, JB)
         store_rows(2)
-        add_two(nc.vector, 3, fresh("two3", tag="biased1"))
+        add_two_biased(3, second[:, 0], (2, 3))
         hand_on(0, 2 * JB)
         store_words(0, 2 * JB)
         add_three(nc.vector, 3, 0, JB // 2)

@@ -230,6 +230,17 @@ def tile_list_dl_soft_geluP_kernel(
                     into[:, t, :], pooled[0, u][:, t, :], bias[:, t : t + 1], pooled[1, u][:, t, :], ADD, ADD
                 )
 
+        def add_three_biased(u):
+            for t in range(PACK):
+                nc.vector.scalar_tensor_tensor(
+                    total[u][:, t, :], pooled[2, u][:, t, :], bias[:, t : t + 1], two[u][:, t, :], ADD, ADD
+                )
+            nc.scalar.activation(
+                y_bf[:, u * JB * PACK : (u + 1) * JB * PACK].rearrange("p (g r t) -> p g t r", r=4, t=PACK),
+                total[u].rearrange("p t (g r) -> p g t r", r=4),
+                GELU,
+            )
+
         def finish_unbiased(engine, u):
             engine.tensor_tensor(total[u], two[u], pooled[2, u], ADD)
             y_f32 = sb("y_f32_%d" % u, [P, PACK, JB], F32)
@@ -252,10 +263,10 @@ def tile_list_dl_soft_geluP_kernel(
                 GELU,
             )
 
-        def store_rows(u):
-            y_f32 = sb("y_f32_%d" % u, [P, PACK, JB], F32)
-            nc.scalar.activation(y_f32[:], total[u], GELU)
-            nc.sync.dma_start(y_rows[:, :, u * JB : (u + 1) * JB], y_f32[:])
+        def store_rows(u, lo, w, queue):
+            y_f32 = sb("y_f32_%d_%d" % (u, lo), [P, PACK, w], F32)
+            nc.scalar.activation(y_f32[:], total[u][:, :, lo : lo + w], GELU)
+            queue.dma_start(y_rows[:, :, u * JB + lo : u * JB + lo + w], y_f32[:])
 
         def hand_on(j0, w):
             nc.vector.quantize_mx(
@@ -268,37 +279,37 @@ def tile_list_dl_soft_geluP_kernel(
             nc.sync.dma_start(y_words[:, j0 : j0 + w], y_codes[:, j0 : j0 + w].bitcast(I32))
 
         first = late[:, 4 * J : 6 * J].rearrange("p (u t j) -> p u t j", u=2, t=PACK)
+        second = late[:, 0 : 4 * J].rearrange("p (u t j) -> p u t j", u=4, t=PACK)
+        for u in (2, 3):
+            total[u] = fresh("total%d" % u)
         pool(0, 0, first[:, 0])
         pool(0, 1, first[:, 1])
         pool(1, 0)
         quantize_x(2)
-        for u in (0, 2, 3):
-            total[u] = fresh("total%d" % u)
-        second = late[:, 0 : 3 * J].rearrange("p (u t j) -> p u t j", u=3, t=PACK)
-        add_two(nc.gpsimd, 0, fresh("two0", tag="xg_bf2"))
         pool(1, 1, second[:, 2])
-        pool(0, 2, second[:, 0])
+        add_two(nc.vector, 0, second[:, 3])
+        add_two(nc.gpsimd, 1, fresh("two1", tag="pooled1_0"))
         pool(2, 0)
-        finish_unbiased(nc.gpsimd, 0)
+        pool(0, 2, second[:, 0])
         pool(2, 1)
+        total[0] = first[:, 1]
+        finish_unbiased(nc.vector, 0)
+        total[1] = second[:, 3]
+        finish_unbiased(nc.gpsimd, 1)
         pool(1, 2)
-        add_two(nc.gpsimd, 1, iw_sb[1, 1][:, :, 0:JB])
+        add_two(nc.gpsimd, 2, fresh("two2"))
         pool(0, 3, second[:, 1])
-        pool(2, 2)
         pool(1, 3)
+        pool(2, 2)
         pool(2, 3)
-        total[1] = iw_sb[1, 1][:, :, JB : 2 * JB]
-        finish_unbiased(nc.vector, 1)
-        add_two_biased(2, second[:, 2], range(PACK))
-        add_two_biased(3, second[:, 0], (0, 1))
-        add_three(nc.vector, 2, 0, JB)
-        store_rows(2)
-        add_two_biased(3, second[:, 0], (2, 3))
+        add_three_biased(2)
+        store_rows(2, 0, JB, nc.sync)
+        add_two_biased(3, second[:, 0], range(PACK))
         hand_on(0, 2 * JB)
         store_words(0, 2 * JB)
         add_three(nc.vector, 3, 0, JB // 2)
         add_three(nc.vector, 3, JB // 2, JB // 2)
-        store_rows(3)
+        store_rows(3, 0, JB, nc.scalar)
         hand_on(2 * JB, JB)
         hand_on(3 * JB, JB // 2)
         hand_on(3 * JB + JB // 2, JB // 2)

@@ -1,6 +1,7 @@
 from contextlib import ExitStack
 
 import concourse.mybir as mybir
+from concourse.masks import make_identity
 
 K, N, T, J = 512, 512, 2048, 512
 PICKS = 3
@@ -19,6 +20,7 @@ FP8X4 = mybir.dt.float8_e4m3fn_x4
 FP4X4 = mybir.dt.float4_e2m1fn_x4
 MULT = mybir.AluOpType.mult
 ADD = mybir.AluOpType.add
+IDENTITY = mybir.ActivationFunctionType.Identity
 GELU = mybir.ActivationFunctionType.Gelu_apprx_tanh
 
 
@@ -50,6 +52,8 @@ def tile_list_dl_soft_geluP_kernel(
             nc.sync.dma_start(x_sb[i][:], x_rows[i])
 
         nc.gpsimd.memset(s4_raw[:].bitcast(I32), 0)
+        ident = sb("ident", [P, P], F32)
+        make_identity(nc, ident[:])
         nc.sync.dma_start(offsets[:], offs)
         nc.scalar.dma_start(w4_raw[:].bitcast(I32), w4_words[0].bitcast(I32))
         nc.scalar.dma_start(s4_raw[0:16, :].bitcast(I32), w4_scales[0].bitcast(I32))
@@ -152,6 +156,8 @@ def tile_list_dl_soft_geluP_kernel(
             base_pass(out, c, t, j0, width)
             delta_pass(out, c, t, j0, width)
 
+        warm = sb("warm", [P, 8], F32)
+        nc.scalar.activation(warm[:, 0:1], wgt_sb[0][:, 0:1], GELU)
         for i in range(2):
             for c in range(PICKS):
                 if i == 0 and c == 0:
@@ -192,7 +198,7 @@ def tile_list_dl_soft_geluP_kernel(
         pooled = {}
         two = {}
         total = {}
-        bank_of = ((4, 5, 1, 4), (6, 7, 0, 5))
+        bank_of = ((4, 5, 6, 7), (6, 7, 2, 0))
         early = [psum.tile([P, 512], F32, name="bank%d" % u) for u in range(4)]
         for u in range(4):
             for t in range(PACK):
@@ -223,23 +229,31 @@ def tile_list_dl_soft_geluP_kernel(
             two[u] = into
             engine.tensor_tensor(into, pooled[0, u], pooled[1, u], ADD)
 
-        def add_two_biased(u, into, slices):
-            two[u] = into
-            for t in slices:
-                nc.vector.scalar_tensor_tensor(
-                    into[:, t, :], pooled[0, u][:, t, :], bias[:, t : t + 1], pooled[1, u][:, t, :], ADD, ADD
-                )
-
-        def add_three_biased(u):
+        def add_bias(u):
             for t in range(PACK):
-                nc.vector.scalar_tensor_tensor(
-                    total[u][:, t, :], pooled[2, u][:, t, :], bias[:, t : t + 1], two[u][:, t, :], ADD, ADD
-                )
-            nc.scalar.activation(
-                y_bf[:, u * JB * PACK : (u + 1) * JB * PACK].rearrange("p (g r t) -> p g t r", r=4, t=PACK),
-                total[u].rearrange("p t (g r) -> p g t r", r=4),
-                GELU,
-            )
+                nc.scalar.activation(pooled[0, u][:, t, :], pooled[0, u][:, t, :], IDENTITY, bias=bias[:, t : t + 1])
+
+        def add_turned(u, bank):
+            turned = psum.tile([P, 512], F32, name="turned", tag=bank)
+            for c in range(2):
+                for t in range(PACK):
+                    nc.tensor.matmul(
+                        turned[:, t * JB : (t + 1) * JB],
+                        pooled[c, u][:, t, :],
+                        ident[:],
+                        start=c == 0 and t == 0,
+                        stop=c == 1 and t == PACK - 1,
+                        is_transpose=True,
+                    )
+            staged = fresh("staged")
+            nc.scalar.copy(staged, turned[:].rearrange("p (t m) -> p t m", t=PACK))
+            return staged
+
+        def turn_back(u, staged, bank):
+            back = psum.tile([P, 512], F32, name="back", tag=bank)
+            for t in range(PACK):
+                nc.tensor.transpose(back[:, t * JB : (t + 1) * JB], staged[:, t, :], ident[:])
+            two[u] = back[:].rearrange("p (t j) -> p t j", t=PACK)
 
         def finish_unbiased(engine, u):
             engine.tensor_tensor(total[u], two[u], pooled[2, u], ADD)
@@ -247,7 +261,10 @@ def tile_list_dl_soft_geluP_kernel(
             for t in range(PACK):
                 nc.scalar.activation(y_f32[:, t, :], total[u][:, t, :], GELU, bias=bias[:, t : t + 1])
             nc.sync.dma_start(y_rows[:, :, u * JB : (u + 1) * JB], y_f32[:])
-            nc.scalar.copy(
+            return y_f32
+
+        def weave_y(copy, u, y_f32):
+            copy(
                 y_bf[:, u * JB * PACK : (u + 1) * JB * PACK].rearrange("p (g r t) -> p g t r", r=4, t=PACK),
                 y_f32[:].rearrange("p t (g r) -> p g t r", r=4),
             )
@@ -280,36 +297,36 @@ def tile_list_dl_soft_geluP_kernel(
 
         first = late[:, 4 * J : 6 * J].rearrange("p (u t j) -> p u t j", u=2, t=PACK)
         second = late[:, 0 : 4 * J].rearrange("p (u t j) -> p u t j", u=4, t=PACK)
-        for u in (2, 3):
+        for u in range(4):
             total[u] = fresh("total%d" % u)
         pool(0, 0, first[:, 0])
         pool(0, 1, first[:, 1])
         pool(1, 0)
         quantize_x(2)
         pool(1, 1, second[:, 2])
-        add_two(nc.vector, 0, second[:, 3])
-        add_two(nc.gpsimd, 1, fresh("two1", tag="pooled1_0"))
+        staged = add_turned(0, "bank0")
+        add_two(nc.gpsimd, 1, fresh("two1"))
+        pool(0, 3, second[:, 1])
+        add_bias(3)
         pool(2, 0)
-        pool(0, 2, second[:, 0])
         pool(2, 1)
-        total[0] = first[:, 1]
-        finish_unbiased(nc.vector, 0)
-        total[1] = second[:, 3]
-        finish_unbiased(nc.gpsimd, 1)
+        turn_back(0, staged, "bank0")
+        weave_y(nc.scalar.copy, 0, finish_unbiased(nc.vector, 0))
+        weave_y(nc.scalar.copy, 1, finish_unbiased(nc.gpsimd, 1))
+        pool(0, 2, second[:, 0])
         pool(1, 2)
         add_two(nc.gpsimd, 2, fresh("two2"))
-        pool(0, 3, second[:, 1])
         pool(1, 3)
         pool(2, 2)
         pool(2, 3)
-        add_three_biased(2)
-        store_rows(2, 0, JB, nc.sync)
-        add_two_biased(3, second[:, 0], range(PACK))
-        hand_on(0, 2 * JB)
-        store_words(0, 2 * JB)
+        y_two = finish_unbiased(nc.vector, 2)
+        add_two(nc.vector, 3, second[:, 0])
         add_three(nc.vector, 3, 0, JB // 2)
         add_three(nc.vector, 3, JB // 2, JB // 2)
         store_rows(3, 0, JB, nc.scalar)
+        weave_y(nc.vector.tensor_copy, 2, y_two)
+        hand_on(0, 2 * JB)
+        store_words(0, 2 * JB)
         hand_on(2 * JB, JB)
         hand_on(3 * JB, JB // 2)
         hand_on(3 * JB + JB // 2, JB // 2)

@@ -301,6 +301,7 @@ def tile_list_dl_soft_geluP_kernel(
             total[u] = fresh("total%d" % u)
         pool(0, 0, first[:, 0])
         pool(0, 1, first[:, 1])
+        add_bias(1)
         pool(1, 0)
         quantize_x(2)
         pool(1, 1, second[:, 2])
@@ -312,7 +313,8 @@ def tile_list_dl_soft_geluP_kernel(
         pool(2, 1)
         turn_back(0, staged, "bank0")
         weave_y(nc.scalar.copy, 0, finish_unbiased(nc.vector, 0))
-        weave_y(nc.scalar.copy, 1, finish_unbiased(nc.gpsimd, 1))
+        add_three(nc.gpsimd, 1, 0, JB)
+        store_rows(1, 0, JB, nc.sync)
         pool(0, 2, second[:, 0])
         pool(1, 2)
         add_two(nc.gpsimd, 2, fresh("two2"))
@@ -320,7 +322,10 @@ def tile_list_dl_soft_geluP_kernel(
         pool(2, 2)
         pool(2, 3)
         y_two = finish_unbiased(nc.vector, 2)
-        add_two(nc.vector, 3, second[:, 0])
+        two[3] = second[:, 0]
+        for lo in (0, JB // 2):
+            half = slice(lo, lo + JB // 2)
+            nc.vector.tensor_tensor(two[3][:, :, half], pooled[0, 3][:, :, half], pooled[1, 3][:, :, half], ADD)
         add_three(nc.vector, 3, 0, JB // 2)
         add_three(nc.vector, 3, JB // 2, JB // 2)
         store_rows(3, 0, JB, nc.scalar)

@@ -8,6 +8,8 @@ PICKS = 3
 P = 128
 PACK = 4
 JB = 128
+QUARTER = (PICKS - 1) * J // 4
+SQUARE = 32
 FLOPS = 2 * 2 * K * N * PICKS * J
 
 F32 = mybir.dt.float32
@@ -55,21 +57,33 @@ def tile_list_dl_soft_geluP_kernel(
         ident = sb("ident", [P, P], F32)
         make_identity(nc, ident[:])
         nc.sync.dma_start(offsets[:], offs)
-        nc.scalar.dma_start(w4_raw[:].bitcast(I32), w4_words[0].bitcast(I32))
+        quarters = sb("quarters", [P, QUARTER], F32)
+        for s in range(4):
+            queue = nc.scalar if s < 3 else nc.sync
+            queue.dma_start(quarters[s:P:4, :], wgt[s:P:4, J + s * QUARTER : J + (s + 1) * QUARTER])
         nc.scalar.dma_start(s4_raw[0:16, :].bitcast(I32), w4_scales[0].bitcast(I32))
         load_wgt(0, 0, JB)
         load_x(0)
         load_wgt(0, JB, J)
-        load_wgt(1)
-        load_wgt(2)
         load_x(1)
+        nc.sync.dma_start(w4_raw[:].bitcast(I32), w4_words[0].bitcast(I32))
         load_x(2)
         load_x(3)
         nc.sync.dma_start(wd_sb[:], wd.rearrange("(p i) n -> p i n", i=PACK))
 
         w4_codes = sb("w4_codes", [P, 2 * N], U8)
         w4_sc = sb("w4_sc", [P, N], U8)
-        nc.vector.tensor_copy(
+        turned_wgt = sb("turned_wgt", [P, QUARTER], F32)
+        nc.vector.transpose(turned_wgt[:], quarters[:])
+        by_quarter = turned_wgt[:].rearrange("p (b h u s) -> p s b h u", h=2, u=4, s=4)
+        for c in range(1, PICKS):
+            repeated = sb("repeated%d" % c, [P, J], F32)
+            nc.vector.tensor_copy(
+                repeated[:].rearrange("p (s b h r) -> p s b h r", s=2, h=2, r=SQUARE // 2),
+                by_quarter[:, 2 * c - 2 : 2 * c, :, :, 0:1].to_broadcast([P, 2, QUARTER // SQUARE, 2, SQUARE // 2]),
+            )
+            nc.vector.transpose(wgt_sb[c], repeated[:])
+        nc.scalar.copy(
             w4_codes[:].bitcast(U16).rearrange("p (t m) -> p t m", t=PACK),
             w4_raw[:].bitcast(U16).rearrange("p (m t) -> p t m", t=PACK),
         )

@@ -8,7 +8,7 @@ PICKS = 3
 P = 128
 PACK = 4
 JB = 128
-QUARTER = (PICKS - 1) * J // 4
+QUARTER = J // 4
 SQUARE = 32
 FLOPS = 2 * 2 * K * N * PICKS * J
 
@@ -57,14 +57,14 @@ def tile_list_dl_soft_geluP_kernel(
         ident = sb("ident", [P, P], F32)
         make_identity(nc, ident[:])
         nc.sync.dma_start(offsets[:], offs)
-        quarters = sb("quarters", [P, QUARTER], F32)
+        quarters = sb("quarters", [P, PICKS - 1, QUARTER], F32)
+        later_wgt = wgt[:, J:].rearrange("p (c s j) -> p c s j", c=PICKS - 1, s=4)
         for s in range(4):
-            queue = nc.scalar if s < 3 else nc.sync
-            queue.dma_start(quarters[s:P:4, :], wgt[s:P:4, J + s * QUARTER : J + (s + 1) * QUARTER])
+            queue = nc.scalar if s < 2 else nc.sync
+            queue.dma_start(quarters[s:P:4], later_wgt[s:P:4, :, s])
         nc.scalar.dma_start(s4_raw[0:16, :].bitcast(I32), w4_scales[0].bitcast(I32))
-        load_wgt(0, 0, JB)
         load_x(0)
-        load_wgt(0, JB, J)
+        load_wgt(0)
         load_x(1)
         nc.sync.dma_start(w4_raw[:].bitcast(I32), w4_words[0].bitcast(I32))
         load_x(2)
@@ -73,14 +73,14 @@ def tile_list_dl_soft_geluP_kernel(
 
         w4_codes = sb("w4_codes", [P, 2 * N], U8)
         w4_sc = sb("w4_sc", [P, N], U8)
-        turned_wgt = sb("turned_wgt", [P, QUARTER], F32)
-        nc.vector.transpose(turned_wgt[:], quarters[:])
-        by_quarter = turned_wgt[:].rearrange("p (b h u s) -> p s b h u", h=2, u=4, s=4)
         for c in range(1, PICKS):
+            turned_wgt = sb("turned_wgt%d" % c, [P, QUARTER], F32)
+            nc.vector.transpose(turned_wgt[:], quarters[:, c - 1, :])
+            by_quarter = turned_wgt[:].rearrange("p (b h u s) -> p s b h u", h=2, u=4, s=4)
             repeated = sb("repeated%d" % c, [P, J], F32)
             nc.vector.tensor_copy(
-                repeated[:].rearrange("p (s b h r) -> p s b h r", s=2, h=2, r=SQUARE // 2),
-                by_quarter[:, 2 * c - 2 : 2 * c, :, :, 0:1].to_broadcast([P, 2, QUARTER // SQUARE, 2, SQUARE // 2]),
+                repeated[:].rearrange("p (s b h r) -> p s b h r", s=4, h=2, r=SQUARE // 2),
+                by_quarter[:, :, :, :, 0:1].to_broadcast([P, 4, QUARTER // SQUARE, 2, SQUARE // 2]),
             )
             nc.vector.transpose(wgt_sb[c], repeated[:])
         nc.scalar.copy(
@@ -171,14 +171,10 @@ def tile_list_dl_soft_geluP_kernel(
             delta_pass(out, c, t, j0, width)
 
         warm = sb("warm", [P, 8], F32)
-        nc.scalar.activation(warm[:, 0:1], wgt_sb[0][:, 0:1], GELU)
+        nc.scalar.activation(warm[:, 0:1], quarters[:, 0, 0:1], GELU)
         for i in range(2):
-            for c in range(PICKS):
-                if i == 0 and c == 0:
-                    gather(c, i, 0, JB)
-                    gather(c, i, JB, J)
-                else:
-                    gather(c, i)
+            for c in (1, 2, 0) if i == 0 else range(PICKS):
+                gather(c, i)
             if i == 0:
                 load_iw(2, 0, "x0")
         load_iw(0, 1, "x1")

@@ -8,6 +8,7 @@ PICKS = 3
 P = 128
 PACK = 4
 JB = 128
+HALF = J // 2
 QUARTER = J // 4
 SQUARE = 32
 FLOPS = 2 * 2 * K * N * PICKS * J
@@ -40,9 +41,13 @@ def tile_list_dl_soft_geluP_kernel(
         offsets = keep.tile([P, PICKS * J // 16], U16, name="offsets")
         x_rows = xT.rearrange("(p i) t -> i p t", i=PACK)
         x_sb = [sb("x%d" % i, [P, T], F32) for i in range(PACK)]
-        late = sb("late", [P, 6 * J], F32)
-        wgt_sb = [late[:, 2 * J : 3 * J]] + [sb("wgt%d" % c, [P, J], F32)[:] for c in range(1, PICKS)]
-        wd_sb = sb("wd", [P, PACK, N], F32)
+        late = sb("late", [P, 24 * HALF], F32)
+
+        def room(lo, hi):
+            return late[:, lo * HALF : hi * HALF]
+
+        wgt_sb = [room(10, 12)] + [sb("wgt%d" % c, [P, J], F32)[:] for c in range(1, PICKS)]
+        wd_sb = room(16, 24).rearrange("p (i n) -> p i n", i=PACK)
         w4_raw = sb("w4_raw", [P, 2 * N], U8)
         s4_raw = sb("s4_raw", [P, N], U8)
         bias = sb("bias", [P, PACK], F32)
@@ -69,7 +74,7 @@ def tile_list_dl_soft_geluP_kernel(
         nc.sync.dma_start(w4_raw[:].bitcast(I32), w4_words[0].bitcast(I32))
         load_x(2)
         load_x(3)
-        nc.sync.dma_start(wd_sb[:], wd.rearrange("(p i) n -> p i n", i=PACK))
+        nc.sync.dma_start(wd_sb, wd.rearrange("(p i) n -> p i n", i=PACK))
 
         w4_codes = sb("w4_codes", [P, 2 * N], U8)
         w4_sc = sb("w4_sc", [P, N], U8)
@@ -109,11 +114,11 @@ def tile_list_dl_soft_geluP_kernel(
         lo1 = sb("lo1", [P, 2, J], F32)
         pairs = {
             (0, 0): lo0[:],
-            (0, 1): late[:, 3 * J : 5 * J].rearrange("p (e j) -> p e j", e=2),
+            (0, 1): room(12, 16).rearrange("p (e j) -> p e j", e=2),
             (1, 0): lo1[:],
-            (1, 1): late[:, 4 * J : 6 * J].rearrange("p (e j) -> p e j", e=2),
+            (1, 1): room(8, 14).rearrange("p (q j) -> p q j", j=J)[:, ::-2],
         }
-        planes2 = late[:, 0 : 4 * J].rearrange("p (i j) -> p i j", i=PACK)
+        planes2 = room(0, 20).rearrange("p (i j) -> p i j", i=PACK)[:, :, 0:J]
         xg_bf = [sb("xg_bf%d" % c, [P, J * PACK], BF16)[:] for c in range(PICKS)]
         xg_codes = [sb("xg_codes%d" % c, [P, J], U32) for c in range(PICKS)]
         xg_sc = [sb("xg_sc%d" % c, [P, J], U8) for c in range(PICKS)]
@@ -190,13 +195,14 @@ def tile_list_dl_soft_geluP_kernel(
         quantize_x(0)
         nc.scalar.copy(
             wd_bf.rearrange("p (t m i) -> p m i t", t=PACK, i=PACK),
-            wd_sb[:].rearrange("p i (m t) -> p m i t", t=PACK),
+            wd_sb.rearrange("p i (m t) -> p m i t", t=PACK),
         )
         gather(1, 2)
         weave_pair(1, 1)
+        gather(2, 3, 0, HALF)
         wd_codes = sb("wd_codes", [P, N], U32)
         nc.vector.quantize_mx(out=wd_codes[:].bitcast(FP8X4), scales=wd_sc[:], in_=wd_bf)
-        gather(2, 3)
+        gather(2, 3, HALF, J)
         weave_all()
         quantize_x(1)
 
@@ -305,12 +311,12 @@ def tile_list_dl_soft_geluP_kernel(
         def store_words(j0, w):
             nc.sync.dma_start(y_words[:, j0 : j0 + w], y_codes[:, j0 : j0 + w].bitcast(I32))
 
-        first = late[:, 4 * J : 6 * J].rearrange("p (u t j) -> p u t j", u=2, t=PACK)
-        second = late[:, 0 : 4 * J].rearrange("p (u t j) -> p u t j", u=4, t=PACK)
+        first = [sb("first%d" % u, [P, PACK, JB], F32, tag=after)[:] for u, after in enumerate(("wgt2", "x3"))]
+        second = planes2.rearrange("p u (t j) -> p u t j", t=PACK)
         for u in range(4):
             total[u] = fresh("total%d" % u)
-        pool(0, 0, first[:, 0])
-        pool(0, 1, first[:, 1])
+        pool(0, 0, first[0])
+        pool(0, 1, first[1])
         add_bias(1)
         pool(1, 0)
         quantize_x(2)

from contextlib import ExitStack

import concourse.mybir as mybir
from concourse.masks import make_identity

K, N, T, J = 512, 512, 2048, 512
PICKS = 3
P = 128
PACK = 4
JB = 128
HALF = J // 2
QUARTER = J // 4
SQUARE = 32
FLOPS = 2 * 2 * K * N * PICKS * J

F32 = mybir.dt.float32
BF16 = mybir.dt.bfloat16
I32 = mybir.dt.int32
U32 = mybir.dt.uint32
U16 = mybir.dt.uint16
U8 = mybir.dt.uint8
FP8X4 = mybir.dt.float8_e4m3fn_x4
FP4X4 = mybir.dt.float4_e2m1fn_x4
MULT = mybir.AluOpType.mult
ADD = mybir.AluOpType.add
IDENTITY = mybir.ActivationFunctionType.Identity
GELU = mybir.ActivationFunctionType.Gelu_apprx_tanh


def tile_list_dl_soft_geluP_kernel(
    tc, xT, wgt, w4_words, w4_scales, wd, iw0, iw1, iw2, b, offs, out_0, out_1, out_2
):
    nc = tc.nc
    with ExitStack() as ctx:
        keep = ctx.enter_context(tc.tile_pool(name="keep", bufs=1))
        psum = ctx.enter_context(tc.psum_pool(name="psum", bufs=1))

        def sb(name, shape, dtype, tag=None):
            return keep.tile(shape, dtype, name=name, tag=tag or name, align_bytes=64)

        offsets = keep.tile([P, PICKS * J // 16], U16, name="offsets")
        x_rows = xT.rearrange("(p i) t -> i p t", i=PACK)
        x_sb = [sb("x%d" % i, [P, T], F32) for i in range(PACK)]
        late = sb("late", [P, 24 * HALF], F32)

        def room(lo, hi):
            return late[:, lo * HALF : hi * HALF]

        wgt_sb = [room(10, 12)] + [sb("wgt%d" % c, [P, J], F32)[:] for c in range(1, PICKS)]
        wd_sb = room(16, 24).rearrange("p (i n) -> p i n", i=PACK)
        w4_raw = sb("w4_raw", [P, 2 * N], U8)
        s4_raw = sb("s4_raw", [P, N], U8)
        bias = sb("bias", [P, PACK], F32)

        def load_wgt(c, lo=0, hi=J):
            nc.sync.dma_start(wgt_sb[c][:, lo:hi], wgt[:, c * J + lo : c * J + hi])

        def load_x(i):
            nc.sync.dma_start(x_sb[i][:], x_rows[i])

        nc.gpsimd.memset(s4_raw[:].bitcast(I32), 0)
        ident = sb("ident", [P, P], F32)
        make_identity(nc, ident[:])
        nc.sync.dma_start(offsets[:], offs)
        quarters = sb("quarters", [P, PICKS - 1, QUARTER], F32)
        later_wgt = wgt[:, J:].rearrange("p (c s j) -> p c s j", c=PICKS - 1, s=4)
        for s in range(4):
            queue = nc.scalar if s < 2 else nc.sync
            queue.dma_start(quarters[s:P:4], later_wgt[s:P:4, :, s])
        nc.scalar.dma_start(s4_raw[0:16, :].bitcast(I32), w4_scales[0].bitcast(I32))
        load_x(0)
        load_wgt(0)
        load_x(1)
        nc.sync.dma_start(w4_raw[:].bitcast(I32), w4_words[0].bitcast(I32))
        load_x(2)
        load_x(3)
        nc.sync.dma_start(wd_sb, wd.rearrange("(p i) n -> p i n", i=PACK))

        w4_codes = sb("w4_codes", [P, 2 * N], U8)
        w4_sc = sb("w4_sc", [P, N], U8)
        for c in range(1, PICKS):
            turned_wgt = sb("turned_wgt%d" % c, [P, QUARTER], F32)
            nc.vector.transpose(turned_wgt[:], quarters[:, c - 1, :])
            by_quarter = turned_wgt[:].rearrange("p (b h u s) -> p s b h u", h=2, u=4, s=4)
            repeated = sb("repeated%d" % c, [P, J], F32)
            nc.vector.tensor_copy(
                repeated[:].rearrange("p (s b h r) -> p s b h r", s=4, h=2, r=SQUARE // 2),
                by_quarter[:, :, :, :, 0:1].to_broadcast([P, 4, QUARTER // SQUARE, 2, SQUARE // 2]),
            )
            nc.vector.transpose(wgt_sb[c], repeated[:])
        nc.scalar.copy(
            w4_codes[:].bitcast(U16).rearrange("p (t m) -> p t m", t=PACK),
            w4_raw[:].bitcast(U16).rearrange("p (m t) -> p t m", t=PACK),
        )
        nc.vector.tensor_copy(
            w4_sc[:].rearrange("p (t m) -> p t m", t=PACK),
            s4_raw[:].rearrange("p (m t) -> p t m", t=PACK),
        )

        for q in range(1, 4):
            nc.sync.dma_start(w4_sc[32 * q : 32 * q + 4, :].bitcast(I32), w4_sc[4 * q : 4 * q + 4, :].bitcast(I32))
        nc.sync.dma_start(bias[:], b.rearrange("(p t) -> p t", t=PACK))
        iw_sb = {}

        def load_iw(c, h, after):
            iw_sb[c, h] = sb("iw%d_%d" % (c, h), [P, PACK, J // 2], F32, tag=after)
            rows = (iw0, iw1, iw2)[c].rearrange("(p t) j -> p t j", t=PACK)
            nc.sync.dma_start(iw_sb[c, h][:], rows[:, :, h * J // 2 : (h + 1) * J // 2])

        load_iw(0, 0, "s4_raw")
        load_iw(1, 0, "w4_raw")

        lo0 = sb("lo0", [P, 2, J], F32)
        lo1 = sb("lo1", [P, 2, J], F32)
        pairs = {
            (0, 0): lo0[:],
            (0, 1): room(12, 16).rearrange("p (e j) -> p e j", e=2),
            (1, 0): lo1[:],
            (1, 1): room(8, 14).rearrange("p (q j) -> p q j", j=J)[:, ::-2],
        }
        planes2 = room(0, 20).rearrange("p (i j) -> p i j", i=PACK)[:, :, 0:J]
        xg_bf = [sb("xg_bf%d" % c, [P, J * PACK], BF16)[:] for c in range(PICKS)]
        xg_codes = [sb("xg_codes%d" % c, [P, J], U32) for c in range(PICKS)]
        xg_sc = [sb("xg_sc%d" % c, [P, J], U8) for c in range(PICKS)]
        wd_bf = sb("wd_bf", [P, N * PACK], BF16)[:]
        wd_sc = sb("wd_sc", [P, N], U8)

        def gather(c, i, lo=0, hi=J):
            into = planes2[:, i, lo:hi] if c == 2 else pairs[c, i // 2][:, i % 2, lo:hi]
            nc.vector.tensor_tensor(
                into,
                x_sb[i][:].indirect(offsets[:, (c * J + lo) // 16 : (c * J + hi) // 16]),
                wgt_sb[c][:, lo:hi],
                MULT,
            )

        def weave_all():
            nc.scalar.copy(
                xg_bf[2].rearrange("p (g r i) -> p g i r", r=4, i=PACK),
                planes2.rearrange("p i (g r) -> p g i r", r=4),
            )

        def weave_pair(c, u):
            nc.scalar.copy(
                xg_bf[c].rearrange("p (j u e) -> p u j e", u=2, e=2)[:, u],
                pairs[c, u].rearrange("p e j -> p j e"),
            )

        def quantize_x(c):
            nc.vector.quantize_mx(out=xg_codes[c][:].bitcast(FP8X4), scales=xg_sc[c][:], in_=xg_bf[c])

        def base_pass(out, c, t, j0, width, start=True):
            nc.tensor.matmul_mx(
                out=out,
                lhsT=w4_codes[:, 2 * P * t : 2 * P * (t + 1)].bitcast(FP4X4),
                lhsT_scale=w4_sc[:, P * t : P * (t + 1)],
                rhs=xg_codes[c][:, j0 : j0 + width].bitcast(FP8X4),
                rhs_scale=xg_sc[c][:, j0 : j0 + width],
                start=start,
                stop=False,
            )

        def delta_pass(out, c, t, j0, width, stop=True):
            nc.tensor.matmul_mx(
                out=out,
                lhsT=wd_codes[:, P * t : P * (t + 1)].bitcast(FP8X4),
                lhsT_scale=wd_sc[:, P * t : P * (t + 1)],
                rhs=xg_codes[c][:, j0 : j0 + width].bitcast(FP8X4),
                rhs_scale=xg_sc[c][:, j0 : j0 + width],
                start=False,
                stop=stop,
            )

        def project(out, c, t, j0, width):
            base_pass(out, c, t, j0, width)
            delta_pass(out, c, t, j0, width)

        warm = sb("warm", [P, 8], F32)
        nc.scalar.activation(warm[:, 0:1], quarters[:, 0, 0:1], GELU)
        for i in range(2):
            for c in (1, 2, 0) if i == 0 else range(PICKS):
                gather(c, i)
            if i == 0:
                load_iw(2, 0, "x0")
        load_iw(0, 1, "x1")
        weave_pair(0, 0)
        weave_pair(1, 0)
        load_iw(1, 1, "lo0")
        load_iw(2, 1, "lo1")
        gather(0, 2)
        gather(0, 3)
        weave_pair(0, 1)
        gather(1, 3)
        gather(2, 2)
        quantize_x(0)
        nc.scalar.copy(
            wd_bf.rearrange("p (t m i) -> p m i t", t=PACK, i=PACK),
            wd_sb.rearrange("p i (m t) -> p m i t", t=PACK),
        )
        gather(1, 2)
        weave_pair(1, 1)
        gather(2, 3, 0, HALF)
        wd_codes = sb("wd_codes", [P, N], U32)
        nc.vector.quantize_mx(out=wd_codes[:].bitcast(FP8X4), scales=wd_sc[:], in_=wd_bf)
        gather(2, 3, HALF, J)
        weave_all()
        quantize_x(1)

        y_sc = sb("y_sc", [P, J], U8)
        y_codes = sb("y_codes", [P, J], U32)
        y_bf = sb("y_bf", [P, J * PACK], BF16)
        y_rows = out_0.rearrange("(p t) j -> p t j", t=PACK)
        y_words = out_1[0].rearrange("p j i -> p (j i)").bitcast(I32)
        pooled = {}
        two = {}
        total = {}
        bank_of = ((4, 5, 6, 7), (6, 7, 2, 0))
        early = [psum.tile([P, 512], F32, name="bank%d" % u) for u in range(4)]
        for u in range(4):
            for t in range(PACK):
                base_pass(early[u][:, t * JB : (t + 1) * JB], 0, t, u * JB, JB, start=t == 0)
        for u in range(4):
            for t in range(PACK):
                delta_pass(early[u][:, t * JB : (t + 1) * JB], 0, t, u * JB, JB, stop=t == PACK - 1)

        def fresh(name, tag=None):
            return sb(name, [P, PACK, JB], F32, tag=tag)[:]

        def pool(c, u, into=None):
            if c == 0:
                acc = early[u]
            else:
                acc = psum.tile([P, 512], F32, name="bank%d" % bank_of[c - 1][u])
                for t in range(PACK):
                    project(acc[:, t * JB : (t + 1) * JB], c, t, u * JB, JB)
            pooled[c, u] = fresh("pooled%d_%d" % (c, u)) if into is None else into
            nc.vector.tensor_tensor(
                pooled[c, u],
                acc[:].rearrange("p (t j) -> p t j", t=PACK),
                iw_sb[c, u // 2][:, :, u % 2 * JB : (u % 2 + 1) * JB],
                MULT,
            )

        def add_two(engine, u, into):
            two[u] = into
            engine.tensor_tensor(into, pooled[0, u], pooled[1, u], ADD)

        def add_bias(u):
            for t in range(PACK):
                nc.scalar.activation(pooled[0, u][:, t, :], pooled[0, u][:, t, :], IDENTITY, bias=bias[:, t : t + 1])

        def add_turned(u, bank):
            turned = psum.tile([P, 512], F32, name="turned", tag=bank)
            for c in range(2):
                for t in range(PACK):
                    nc.tensor.matmul(
                        turned[:, t * JB : (t + 1) * JB],
                        pooled[c, u][:, t, :],
                        ident[:],
                        start=c == 0 and t == 0,
                        stop=c == 1 and t == PACK - 1,
                        is_transpose=True,
                    )
            staged = fresh("staged")
            nc.scalar.copy(staged, turned[:].rearrange("p (t m) -> p t m", t=PACK))
            return staged

        def turn_back(u, staged, bank):
            back = psum.tile([P, 512], F32, name="back", tag=bank)
            for t in range(PACK):
                nc.tensor.transpose(back[:, t * JB : (t + 1) * JB], staged[:, t, :], ident[:])
            two[u] = back[:].rearrange("p (t j) -> p t j", t=PACK)

        def finish_unbiased(engine, u):
            engine.tensor_tensor(total[u], two[u], pooled[2, u], ADD)
            y_f32 = sb("y_f32_%d" % u, [P, PACK, JB], F32)
            for t in range(PACK):
                nc.scalar.activation(y_f32[:, t, :], total[u][:, t, :], GELU, bias=bias[:, t : t + 1])
            nc.sync.dma_start(y_rows[:, :, u * JB : (u + 1) * JB], y_f32[:])
            return y_f32

        def weave_y(copy, u, y_f32):
            copy(
                y_bf[:, u * JB * PACK : (u + 1) * JB * PACK].rearrange("p (g r t) -> p g t r", r=4, t=PACK),
                y_f32[:].rearrange("p t (g r) -> p g t r", r=4),
            )

        def add_three(engine, u, lo, w):
            j0 = u * JB + lo
            engine.tensor_tensor(
                total[u][:, :, lo : lo + w], two[u][:, :, lo : lo + w], pooled[2, u][:, :, lo : lo + w], ADD
            )
            nc.scalar.activation(
                y_bf[:, j0 * PACK : (j0 + w) * PACK].rearrange("p (g r t) -> p g t r", r=4, t=PACK),
                total[u][:, :, lo : lo + w].rearrange("p t (g r) -> p g t r", r=4),
                GELU,
            )

        def store_rows(u, lo, w, queue):
            y_f32 = sb("y_f32_%d_%d" % (u, lo), [P, PACK, w], F32)
            nc.scalar.activation(y_f32[:], total[u][:, :, lo : lo + w], GELU)
            queue.dma_start(y_rows[:, :, u * JB + lo : u * JB + lo + w], y_f32[:])

        def hand_on(j0, w):
            nc.vector.quantize_mx(
                out=y_codes[:, j0 : j0 + w].bitcast(FP8X4),
                scales=y_sc[:, j0 : j0 + w],
                in_=y_bf[:, j0 * PACK : (j0 + w) * PACK],
            )

        def store_words(j0, w):
            nc.sync.dma_start(y_words[:, j0 : j0 + w], y_codes[:, j0 : j0 + w].bitcast(I32))

        first = [sb("first%d" % u, [P, PACK, JB], F32, tag=after)[:] for u, after in enumerate(("wgt2", "x3"))]
        second = planes2.rearrange("p u (t j) -> p u t j", t=PACK)
        for u in range(4):
            total[u] = fresh("total%d" % u)
        pool(0, 0, first[0])
        pool(0, 1, first[1])
        add_bias(1)
        pool(1, 0)
        quantize_x(2)
        pool(1, 1, second[:, 2])
        staged = add_turned(0, "bank0")
        add_two(nc.gpsimd, 1, fresh("two1"))
        pool(0, 3, second[:, 1])
        add_bias(3)
        pool(2, 0)
        pool(2, 1)
        turn_back(0, staged, "bank0")
        weave_y(nc.scalar.copy, 0, finish_unbiased(nc.vector, 0))
        add_three(nc.gpsimd, 1, 0, JB)
        store_rows(1, 0, JB, nc.sync)
        pool(0, 2, second[:, 0])
        pool(1, 2)
        add_two(nc.gpsimd, 2, fresh("two2"))
        pool(1, 3)
        pool(2, 2)
        pool(2, 3)
        y_two = finish_unbiased(nc.vector, 2)
        two[3] = second[:, 0]
        for lo in (0, JB // 2):
            half = slice(lo, lo + JB // 2)
            nc.vector.tensor_tensor(two[3][:, :, half], pooled[0, 3][:, :, half], pooled[1, 3][:, :, half], ADD)
        add_three(nc.vector, 3, 0, JB // 2)
        add_three(nc.vector, 3, JB // 2, JB // 2)
        store_rows(3, 0, JB, nc.scalar)
        weave_y(nc.vector.tensor_copy, 2, y_two)
        hand_on(0, 2 * JB)
        store_words(0, 2 * JB)
        hand_on(2 * JB, JB)
        hand_on(3 * JB, JB // 2)
        hand_on(3 * JB + JB // 2, JB // 2)
        store_words(2 * JB, 2 * JB)
        for q in range(4):
            queue = nc.scalar if q % 2 else nc.sync
            queue.dma_start(out_2[0, 4 * q : 4 * q + 4, :].bitcast(I32), y_sc[32 * q : 32 * q + 4, :].bitcast(I32))
